import numpy as np, ml_dtypes
CORES = [24,48,72,152,176,200]
N = 6
R, KR, T = 8192, 131072, 2048
CAPP = 512
def entries(a): return a.T.reshape(-1)
def pack(v, P): return np.ascontiguousarray(np.asarray(v, np.int32).reshape(-1, P).T)
def owners(rng, n, cap):
    return np.stack([rng.permutation(np.repeat(np.arange(N), cap))[:n] for r in range(N)])
def lists(rng, how):
    K = rng.permutation(N * KR)[:N * R]
    G = R * owners(rng, T, CAPP) + rng.integers(0, R, (N, T))
    if how == "uniform": G[:, :T // 8] = -1
    if how == "alike": O = np.stack([np.repeat(rng.permutation(N)[:T // CAPP], CAPP) for r in range(N)]); G = R * O + rng.integers(0, R, N)[O]
    if how == "edge":
        en = np.concatenate([KR * np.arange(N), KR * np.arange(N) + KR - 1]); ep = np.concatenate([R * np.arange(N), R * np.arange(N) + R - 1])
        K = rng.permutation(np.setdiff1d(np.arange(N * KR), en))[:N * R]; K[ep] = rng.permutation(en)
        G = np.concatenate([np.tile(ep, (N, 1)), R * owners(rng, T - 2 * N, CAPP - 2) + rng.integers(0, R, (N, T - 2 * N))], axis=1)
    if how == "full":
        lo = KR * int(rng.integers(N)) + int(rng.integers(T // 2, KR - N * R - T // 2 + 1)); K = lo + rng.permutation(N * R); rp = rng.permutation(N)
        G = np.stack([np.concatenate([R * h + rng.permutation(R)[:CAPP] for h in rp[:T // CAPP]]) for r in range(N)]); G[int(rng.integers(N)), :CAPP] = -1
    if how == "own":
        m = min(32, KR // R); c = int(rng.integers(m)); q = np.stack([rng.permutation(np.concatenate([2 * rng.permutation(KR // (2 * m))[:R // 2], 2 * rng.permutation(KR // (2 * m))[:R // 2] + 1])) for r in range(N)])
        pp = KR * ((np.arange(N) + int(rng.integers(1, N))) % N)[:, None] + m * q
        K = (pp + c).reshape(-1); O = (np.arange(N)[:, None] + 1 + np.arange(T) // 2 % (N - 1)) % N; O[:, :CAPP] = np.arange(N)[:, None]
        ev = np.stack([np.nonzero(v % 2 == 0)[0] for v in q]); G = R * O + ev[O, rng.integers(0, R // 2, (N, T))]; G[:, CAPP::2] = -1
    F = np.setdiff1d(np.arange(N * KR), K); Z = F[rng.integers(0, len(F), (N, T))]
    if how == "full": Z = np.tile(np.where(np.arange(T) % 2 == 0, lo - 1 - np.arange(T) // 2, lo + N * R + np.arange(T) // 2), (N, 1))
    if how == "own": Z = np.take_along_axis(pp, rng.integers(0, R, (N, T)), axis=1) + (c + rng.integers(1, m, (N, T))) % m
    if how == "absent":
        G[:, :T // 3] = -1; G[int(rng.integers(N))] = -1
        for j, d in ((0, 1), (1, -1)): nb = np.intersect1d(K + d, F); Z[:, j::4] = nb[rng.integers(0, len(nb), (N, T // 4))]
    W = np.where(G >= 0, K[np.maximum(G, 0)], Z); W = np.take_along_axis(W, np.argsort(rng.random((N, T)), axis=1), axis=1)
    return {"kb": np.stack([pack(k, 16) for k in K.reshape(N, R)]), "ka": np.stack([pack(w, 16) for w in W])}
def setup_inputs(rng):
    return dict({"tab": rng.standard_normal((N, 128, R), dtype=np.float32).astype(ml_dtypes.bfloat16)}, **lists(rng, "uniform"))
def setup_inputs_absent(rng):
    d = setup_inputs(rng); d.update(lists(rng, "absent"))
    for k in ("tab",): d[k] = (d[k].astype(np.float32) * 1048576.0).astype(d[k].dtype)
    return d
def setup_inputs_alike(rng):
    d = setup_inputs(rng); d.update(lists(rng, "alike"))
    for k in ("tab",): d[k] = (d[k].astype(np.float32) * (1 / 1024.0)).astype(d[k].dtype)
    return d
def setup_inputs_edge(rng):
    d = setup_inputs(rng); d.update(lists(rng, "edge"))
    return d
def setup_inputs_full(rng):
    d = setup_inputs(rng); d.update(lists(rng, "full"))
    return d
def setup_inputs_own(rng):
    d = setup_inputs(rng); d.update(lists(rng, "own"))
    return d
def check_inputs(x):
    bad = []
    if x["kb"].min() < 0 or x["kb"].max() >= N * KR: bad.append("kb out of range")
    if x["ka"].min() < 0 or x["ka"].max() >= N * KR: bad.append("ka out of range")
    if bad: return bad
    K = np.concatenate([entries(k) for k in x["kb"]]); H = np.full(N * KR, N); H[K] = np.arange(N * R) // R
    if len(np.unique(K)) < N * R: bad.append("a key stands twice in kb")
    if max(int(np.bincount(H[entries(a)], minlength=N + 1)[:N].max()) for a in x["ka"]) > CAPP: bad.append("more than CAPP entries of a list have their columns on one rank")
    return bad
def reference(tab, kb, ka):
    A = np.concatenate(list(tab) + [np.zeros((128, 1), tab.dtype)], axis=1)
    K, Q = np.concatenate([entries(k) for k in kb]), np.stack([entries(q) for q in ka])
    P = np.full(N * KR, N * R); P[K] = np.arange(N * R)
    return {"y": np.stack([A[:, P[Q[r]]] for r in range(N)])}

@@ -1,0 +1,428 @@
+from concourse.bass import DstId, RemoteDMATransfer
+from concourse.mybir import dt, AluOpType, AxisListType, ActivationFunctionType
+
+A = AluOpType
+AF = ActivationFunctionType
+NR = 6
+NQ = 4
+NT = 16
+NS = 3
+NV = NT - NS
+NH = 12
+CAP = 512
+ZC = NR * CAP
+SL = 5
+NE = 4
+
+SCRATCH = {
+    "qd": ("dram", [128, 16], "int32"),
+    "kd": ("dram", [128, 16], "int32"),
+    "kbs": ("dram", [4, 128, 16], "int32"),
+    "maps": ("dram", [6, 128, 16], "float32"),
+    "Qi": ("sbuf", [128, 16], "int32"),
+    "Ki": ("sbuf", [128, 16], "int32"),
+    "iota12": ("sbuf", [128, 12], "float32"),
+    "pI": ("sbuf", [128, 16], "int32"),
+    "pab": ("sbuf", [128, 32], "int32"),
+    "fab": ("sbuf", [128, 32], "float32"),
+    "cv": ("sbuf", [128, 80], "float32"),
+    "ones": ("sbuf", [128, 128], "bfloat16"),
+    "o256": ("sbuf", [128, 128], "bfloat16"),
+    "ident": ("sbuf", [128, 128], "bfloat16"),
+    "kk": ("sbuf", [128, 32], "int32"),
+    "kf": ("sbuf", [128, 32], "float32"),
+    "qq": ("sbuf", [128, 48], "int32"),
+    "qf": ("sbuf", [128, 48], "float32"),
+    "cls": ("sbuf", [128, NV * NH], "float16"),
+    "cs": ("sbuf", [128, 2 * NS * NH], "bfloat16"),
+    "dl": ("sbuf", [128, 2048], "bfloat16"),
+    "dh": ("sbuf", [128, 2048], "bfloat16"),
+    "qu": ("sbuf", [128, 2048], "uint16"),
+    "mv": ("sbuf", [128, 4 * NV * 512], "float16"),
+    "ma": ("sbuf", [128, 4 * NS * 512], "bfloat16"),
+    "ms": ("sbuf", [128, 4 * NS * 512], "bfloat16"),
+    "mask": ("sbuf", [128, 192], "float32"),
+    "prod": ("sbuf", [128, 192], "float32"),
+    "p1": ("sbuf", [128, 96], "float32"),
+    "p2": ("sbuf", [128, 48], "float32"),
+    "p3": ("sbuf", [128, 64], "float32"),
+    "win": ("sbuf", [128, 8192], "bfloat16"),
+    "codes": ("sbuf", [128, 128], "float32"),
+    "nones": ("sbuf", [128, 128], "bfloat16"),
+    "m1": ("sbuf", [128, 128], "bfloat16"),
+    "zer": ("sbuf", [128, 16], "bfloat16"),
+    "iota32": ("sbuf", [128, 32], "float32"),
+    "iotap": ("sbuf", [128, 128], "float32"),
+    "h2": ("sbuf", [128, 64], "float32"),
+    "G": ("sbuf", [128, 32], "float32"),
+    "F": ("sbuf", [128, 32], "bfloat16"),
+    "inc": ("sbuf", [128, 32], "bfloat16"),
+    "si": ("sbuf", [128, 96], "int32"),
+    "sf": ("sbuf", [128, 64], "float32"),
+    "c1": ("sbuf", [128, 32], "float32"),
+    "smap": ("sbuf", [128, 32], "float32"),
+    "lh": ("sbuf", [128, 4096], "float32"),
+    "la2": ("sbuf", [128, 2 * SL * 128], "float32"),
+    "rh": ("sbuf", [128, 1024], "float32"),
+    "off": ("sbuf", [128, 64], "uint16"),
+    "gb": ("sbuf", [128, 1024], "bfloat16"),
+    "ywin": ("sbuf", [128, ZC + 16], "bfloat16"),
+    "msb": ("sbuf", [96, 128], "float32"),
+    "yoff": ("sbuf", [128, 128], "uint16"),
+    "ysb": ("sbuf", [128, 2048], "bfloat16"),
+}
+for _i in range(4):
+    SCRATCH["q%d" % _i] = ("psum", [128, 512], "float32")
+    SCRATCH["r%d" % _i] = ("psum", [128, 512], "float32")
+SEMAPHORES = ["la", "lb", "go", "t0", "t1", "fwd", "qar", "kar", "kl", "ql", "cod0", "cod1", "tabs", "map", "om",
+              "ml", "dat", "ls", "gs", "vs", "ss", "ps", "sy", "sa"]
+
+
+def low_bits(mask, n, start=0):
+    bits = [1 << i for i in range(16) if mask >> i & 1]
+    return sum(bits[start:start + n])
+
+
+def n_bits(mask):
+    return sum(mask >> i & 1 for i in range(16))
+
+
+def plan(T, topo, ncores=256):
+    cores = list(T.cores)
+    chips = {}
+    where = {}
+    for c in range(ncores):
+        where[c] = (topo.host(c), topo.chip(c))
+        chips.setdefault(where[c], []).append(c)
+    used = set(where[c] for c in cores)
+    match, gat, jobs, helper = {}, {}, {}, {}
+    for s in range(NR):
+        near = [k for k in chips if k not in used and topo.same_plane(cores[s], chips[k][0])]
+        near.sort(key=lambda k: (k[0] != topo.host(cores[s]), abs(k[1] - topo.chip(cores[s])), k[1]))
+        for b, k in enumerate(near[:3]):
+            used.add(k)
+            for i in range(8):
+                match[(s, 2 * b + i // 4, i % 4)] = chips[k][i]
+    for s in range(NR):
+        c0 = cores[s]
+        far = next(c for c in range(ncores) if topo.mates(c0, c))
+        port = [c for c in chips[where[c0]] if c != c0 and topo.may_write(c, far)]
+        ha = next(c for c in port if topo.die(c) == topo.die(c0))
+        hb = next(c for c in port if topo.die(c) != topo.die(c0))
+        helper[s] = (ha, hb)
+        order = [(s + d) % NR for d in range(1, NR)]
+        sp = [r for r in order if topo.same_plane(c0, cores[r])]
+        rest = sp[1:] + [r for r in order if r not in sp]
+        jobs[c0] = (s, [sp[0], s])
+        jobs[ha] = (s, [rest[0], rest[2]])
+        jobs[hb] = (s, [rest[1], rest[3]])
+        for c in (c0, ha, hb):
+            for n, r in enumerate(jobs[c][1]):
+                gat[(s, r)] = (c, n)
+    return cores, match, gat, jobs, helper
+
+
+def rank_program(g, core, T, topo):
+    cores, match, gat, jobs, helper = plan(T, topo)
+    role = next((key for key in match if match[key] == core), None)
+    if role is None and core not in jobs:
+        return
+    queues = {"g": g, "V": g.vector, "S": g.scalar, "P": g.tensor, "Y": g.sync}
+    cnt, seen = {}, {}
+
+    def did(inst, sem, n=1):
+        inst.then_inc(T.sem[sem], n)
+        cnt[sem] = cnt.get(sem, 0) + n
+        return cnt[sem]
+
+    def wait(q, sem, n):
+        if seen.get((q, sem), 0) < n:
+            seen[(q, sem)] = n
+            queues[q].wait_ge(T.sem[sem], n)
+
+    def addr(d):
+        rid, pid = topo.addr(d, core)
+        return DstId(rid=rid, pnc=pid)
+
+    def send(sets, sem):
+        g.remote_dma_fused([RemoteDMATransfer(dst_ids=[addr(d) for d in ds], dma_engine_mask=m, remote_sem=T.sem[sem],
+                                              srcs=[src], dsts=[dst for d in ds], alu_op=0)
+                            for src, dst, ds, m in sets], local_sem=T.sem.ls)
+        cnt["ls"] = cnt.get("ls", 0) + sum(n_bits(m) for src, dst, ds, m in sets)
+
+    if role is not None:
+        run_match(g, core, T, topo, role, gat, did, wait, send)
+    else:
+        run_rank(g, core, T, topo, cores, match, gat, jobs, helper, did, wait, send)
+    for sem in sorted(cnt):
+        wait("g", sem, cnt[sem])
+
+
+def run_rank(g, core, T, topo, cores, match, gat, jobs, helper, did, wait, send):
+    V, S, PE, SY = g.vector, g.scalar, g.tensor, g.sync
+    s, asked = jobs[core]
+    is_rank = core == cores[s]
+    ha, hb = helper[s]
+    did(g.iota(T.iota32[:], [[1, 32]], 0, 0, allow_small_or_imprecise_dtypes=True), "gs")
+    gi = did(g.iota(T.iotap[:], [[0, 8], [1, 16]], 0, 0, allow_small_or_imprecise_dtypes=True), "gs")
+    did(V.memset(T.ones[:], 1.0), "vs")
+    did(V.memset(T.zer[:], 0.0), "vs")
+    vn = did(V.memset(T.nones[:], -1.0), "vs")
+    if is_rank:
+        did(V.memset(T.ywin[:, ZC:ZC + 16], 0.0), "vs")
+        did(SY.dma_start(T.qd[:], T.ka[:]), "la", 16)
+        for q in range(NQ):
+            did(S.dma_start(T.kbs[q], T.kb[:, 128 * q:128 * q + 128]), "lb", 16)
+        wait("g", "la", 16)
+        on = topo.mask(core, ha)
+        send([(T.qd[:], T.qd[:], [ha, hb], low_bits(on, NE))], "fwd")
+        wait("g", "lb", 64)
+        off = topo.mask(core, match[(s, s, 0)])
+        send([(T.kbs[q], T.kd[:], [match[(s, r, q)] for r in range(NR)], low_bits(off, 2, 2 * q)) for q in range(NQ)], "kar")
+        near = [match[(o, s, q)] for o in range(NR) if topo.may_write(core, cores[o]) for q in range(NQ)]
+        send([(T.qd[:], T.qd[:], near, off)], "qar")
+        g.sem_inc(T.sem.go, 1)
+        SY.wait_ge(T.sem.go, 1)
+        did(SY.dma_start(T.win[:, 0:4096], T.tab[:, 0:4096]), "t0", 16)
+        did(SY.dma_start(T.win[:, 4096:8192], T.tab[:, 4096:8192]), "t1", 16)
+        for h in range(2):
+            wait("g", "t%d" % h, 16)
+            w = T.win[:, 4096 * h:4096 * h + 4096]
+            send([(w, w, [ha, hb], on)], "tabs")
+        did(g.iota(T.pI[:], [[0, 16]], 0, 1), "gs")
+    wait("g", "vs", vn)
+    gm = did(g.affine_select(T.m1[:], T.nones[:], [[-1, 128]], A.is_ge, 0.0, 0, 1), "gs")
+    if is_rank:
+        wait("V", "gs", gm)
+        k = did(V.tensor_scalar(T.pab[:, 0:16], T.pI[:], 15, None, A.bitwise_and), "vs")
+        wait("V", "vs", k)
+        k = did(V.tensor_copy(T.fab[:, 0:16], T.pab[:, 0:16]), "vs")
+        wait("V", "vs", k)
+        rep = T.la2[:, 0:128] if False else T.cvrep[:] if False else T.mask[:, 0:128]
+        vrep = did(V.tensor_scalar(rep, T.iotap[:], T.fab[:, 0:1], None, A.is_equal), "vs")
+    else:
+        me = (ha, hb).index(core)
+        cross = [o for o in range(NR) if not topo.may_write(cores[s], cores[o])]
+        mine = cross[me * len(cross) // 2:(me + 1) * len(cross) // 2]
+        dsts = [match[(o, s, q)] for o in mine for q in range(NQ)]
+        wait("g", "fwd", NE)
+        send([(T.qd[:], T.qd[:], dsts, topo.mask(core, dsts[0]))], "qar")
+    wait("P", "gs", gm)
+    wait("P", "vs", vn)
+    wait("V", "gs", gm)
+    wait("S", "gs", gm)
+    for n, r in enumerate(asked):
+        wait("V", "cod%d" % n, NQ * n_bits(topo.mask(match[(s, r, 0)], core)))
+        c = 16 * n
+        G, F, inc, c1, sm = [t[:, c:c + 16] for t in (T.G, T.F, T.inc, T.c1, T.smap)]
+        h2 = T.h2[:, 32 * n:32 * n + 32]
+        k = did(V.tensor_tensor(h2, T.codes[:, 64 * n:64 * n + 32], T.codes[:, 64 * n + 32:64 * n + 64], A.add), "vs")
+        wait("V", "vs", k)
+        k = did(V.tensor_tensor(G, T.h2[:, 32 * n:32 * n + 16], T.h2[:, 32 * n + 16:32 * n + 32], A.add), "vs")
+        wait("V", "vs", k)
+        k = did(V.tensor_scalar(F, G, 0.0, None, A.is_gt), "vs")
+        wait("V", "vs", k)
+        k = did(V.tensor_tensor_scan(inc, F, T.zer[:], 0.0, A.add, A.add), "vs")
+        wait("P", "vs", k)
+        slot = T["q%d" % n][:, 0:16]
+        did(PE.matmul(slot, T.m1[:], F, True, False), "ps")
+        p = did(PE.matmul(slot, T.ones[:], inc, False, True), "ps")
+        wait("V", "ps", p)
+        si = T.si[:, 48 * n:48 * n + 16]
+        k1 = did(V.tensor_copy(si, slot), "vs")
+        k2 = did(V.tensor_scalar(c1, slot, float(CAP * s - ZC), None, A.add), "vs")
+        wait("V", "vs", k1)
+        did(V.tensor_scalar(T.si[:, 48 * n + 16:48 * n + 32], si, 15, None, A.bitwise_and), "vs")
+        k3 = did(V.tensor_scalar(T.si[:, 48 * n + 32:48 * n + 48], si, 4, None, A.arith_shift_right), "vs")
+        wait("V", "vs", k2)
+        km = did(V.tensor_tensor(sm, c1, F, A.mult), "vs")
+        wait("V", "vs", k3)
+        kf = did(V.tensor_copy(T.sf[:, 32 * n:32 * n + 32], T.si[:, 48 * n + 16:48 * n + 48]), "vs")
+        wait("V", "vs", kf)
+        if r == s:
+            wait("Y", "vs", km)
+            did(SY.dma_start(T.maps[s], sm), "om", 16)
+        else:
+            wait("g", "vs", km)
+            send([(sm, T.maps[s], [cores[r]], topo.mask(core, cores[r]))], "map")
+        wait("S", "vs", kf)
+        lst = T["r%d" % n][:, 0:32]
+        tv, ts = {}, {}
+        for t in range(NT):
+            lo, hi = T.sf[:, 32 * n + t:32 * n + t + 1], T.sf[:, 32 * n + 16 + t:32 * n + 17 + t]
+            lh = T.lh[:, 2048 * n + 128 * t:2048 * n + 128 * t + 128]
+            if t >= NT - SL:
+                i = (n * SL + t - NT + SL) * 128
+                a = did(S.activation(T.la2[:, i:i + 128], T.iotap[:], AF.Abs, bias=lo, scale=-1.0), "ss")
+                wait("S", "ss", a)
+                ts[t] = did(S.activation(lh, T.la2[:, i:i + 128], AF.Relu, bias=1.0, scale=-1.0), "ss")
+            else:
+                did(V.tensor_scalar(lh, T.iotap[:], lo, None, A.is_equal), "vs")
+            tv[t] = did(V.tensor_scalar(T.rh[:, 512 * n + 32 * t:512 * n + 32 * t + 32], T.iota32[:], hi,
+                                        T.G[:, c + t:c + t + 1], A.is_equal, A.mult), "vs")
+        for t in range(NT):
+            wait("P", "vs", tv[t])
+            if t in ts:
+                wait("P", "ss", ts[t])
+            p = did(PE.matmul(lst, T.lh[:, 2048 * n + 128 * t:2048 * n + 128 * t + 128],
+                              T.rh[:, 512 * n + 32 * t:512 * n + 32 * t + 32], t == 0, t == NT - 1), "ps")
+        wait("V", "ps", p)
+        k = did(V.tensor_scalar(T.off[:, 32 * n:32 * n + 32], lst, -1.0, None, A.add), "vs")
+        for q in ("V", "S"):
+            wait(q, "vs", k)
+            if is_rank:
+                wait(q, "t0", 16)
+                wait(q, "t1", 16)
+            else:
+                wait(q, "tabs", 2 * n_bits(topo.mask(cores[s], core)))
+        out = T.ywin if r == s else T.gb
+        o = CAP * s if r == s else CAP * n
+        kv = did(V.tensor_copy(out[:, o:o + 256], T.win[:, 0:8192].indirect(T.off[:, 32 * n:32 * n + 16])), "vs")
+        ks = did(S.activation(out[:, o + 256:o + 512], T.win[:, 0:8192].indirect(T.off[:, 32 * n + 16:32 * n + 32]), AF.Copy), "ss")
+        if r != s:
+            wait("g", "vs", kv)
+            wait("g", "ss", ks)
+            send([(T.gb[:, o:o + CAP], T.ywin[:, CAP * s:CAP * s + CAP], [cores[r]], topo.mask(core, cores[r]))], "dat")
+    if not is_rank:
+        return
+    tot = sum(n_bits(topo.mask(gat[(o, s)][0], core)) for o in range(NR) if o != s)
+    wait("Y", "map", tot)
+    wait("Y", "om", 16)
+    did(SY.dma_start(T.msb[:], T.maps[:]), "ml", 16)
+    wait("P", "ml", 16)
+    wait("P", "vs", vrep)
+    p = did(PE.matmul(T.q2[:, 0:128], T.mask[0:96, 0:128], T.msb[:], True, True), "ps")
+    wait("V", "ps", p)
+    k = did(V.tensor_scalar(T.yoff[:], T.q2[:, 0:128], float(ZC), None, A.add), "vs")
+    for q in ("V", "S"):
+        wait(q, "vs", k)
+        wait(q, "ss", ks)
+        wait(q, "dat", tot)
+    last = []
+    for h in range(2):
+        a = 512 * h
+        k = did(V.tensor_copy(T.ysb[:, a:a + 512], T.ywin[:, 0:ZC + 16].indirect(T.yoff[:, 32 * h:32 * h + 32])), "vs")
+        wait("Y", "vs", k)
+        did(SY.dma_start(T.y[:, a:a + 512], T.ysb[:, a:a + 512]), "sy", 16)
+        b = 1024 + a
+        last.append(did(S.activation(T.ysb[:, b:b + 512], T.ywin[:, 0:ZC + 16].indirect(T.yoff[:, 64 + 32 * h:96 + 32 * h]), AF.Copy), "ss"))
+    for h in range(2):
+        b = 1024 + 512 * h
+        wait("S", "ss", last[h])
+        did(S.dma_start(T.y[:, b:b + 512], T.ysb[:, b:b + 512]), "sa", 16)
+
+
+def run_match(g, core, T, topo, role, gat, did, wait, send):
+    s, r, q = role
+    V, S, PE, SY = g.vector, g.scalar, g.tensor, g.sync
+    a256, v16, b1, val, tt = [T.cv[:, 16 * i:16 * i + 16] for i in range(5)]
+    did(g.iota(T.iota12[:], [[1, 12]], 0, 0, allow_small_or_imprecise_dtypes=True), "gs")
+    did(g.iota(T.pI[:], [[0, 16]], 0, 1), "gs")
+    gi = did(g.iota(tt, [[16, 16]], 0, 0, allow_small_or_imprecise_dtypes=True), "gs")
+    k = did(V.memset(T.ones[:], 1.0), "vs")
+    did(V.memset(T.o256[:], 256.0), "vs")
+    wait("g", "vs", k)
+    gd = did(g.affine_select(T.ident[:], T.ones[:], [[-1, 128]], A.is_equal, 0.0, 0, 1), "gs")
+    wait("V", "gs", gi)
+    did(V.tensor_scalar(T.pab[:, 0:16], T.pI[:], 7, None, A.bitwise_and), "vs")
+    k = did(V.tensor_scalar(T.pab[:, 16:32], T.pI[:], 3, None, A.arith_shift_right), "vs")
+    wait("V", "vs", k)
+    k = did(V.tensor_copy(T.fab[:], T.pab[:]), "vs")
+    wait("V", "vs", k)
+    did(V.tensor_scalar(a256, T.fab[:, 0:16], 256.0, None, A.mult), "vs")
+    k = did(V.tensor_scalar(b1, T.fab[:, 16:32], 1.0, None, A.add), "vs")
+    wait("V", "vs", k)
+    k = did(V.tensor_tensor(v16, a256, tt, A.add), "vs")
+    wait("V", "vs", k)
+    k = did(V.tensor_tensor(val, v16, b1, A.add), "vs")
+    wait("V", "vs", k)
+    wait("Y", "kar", 2)
+    did(SY.dma_start(T.Ki[:], T.kd[:]), "kl", 16)
+    wait("S", "qar", n_bits(topo.mask(T.cores[s], core)))
+    did(S.dma_start(T.Qi[:], T.qd[:]), "ql", 16)
+    wait("V", "kl", 16)
+    did(V.tensor_scalar(T.kk[:, 0:16], T.Ki[:], 65535, None, A.bitwise_and), "vs")
+    k = did(V.tensor_scalar(T.kk[:, 16:32], T.Ki[:], 16, None, A.arith_shift_right), "vs")
+    wait("V", "vs", k)
+    k = did(V.tensor_copy(T.kf[:], T.kk[:]), "vs")
+    wait("V", "vs", k)
+    for t in range(NT):
+        hi = T.kf[:, 16 + t:17 + t]
+        if t < NV:
+            did(V.tensor_scalar(T.cls[:, NH * t:NH * t + NH], T.iota12[:], hi, T.cv[:, 48 + t:49 + t], A.is_equal, A.mult), "vs")
+        else:
+            i = 2 * NH * (t - NV)
+            did(V.tensor_scalar(T.cs[:, i:i + NH], T.iota12[:], hi, T.cv[:, 16 + t:17 + t], A.is_equal, A.mult), "vs")
+            did(V.tensor_scalar(T.cs[:, i + NH:i + 2 * NH], T.iota12[:], hi, T.cv[:, 32 + t:33 + t], A.is_equal, A.mult), "vs")
+    wait("V", "ql", 16)
+    did(V.tensor_scalar(T.qq[:, 0:16], T.Qi[:], 255, None, A.bitwise_and), "vs")
+    did(V.tensor_scalar(T.qq[:, 16:32], T.Qi[:], 8, 255, A.arith_shift_right, A.bitwise_and), "vs")
+    k = did(V.tensor_scalar(T.qq[:, 32:48], T.Qi[:], 16, None, A.arith_shift_right), "vs")
+    wait("V", "vs", k)
+    kq = did(V.tensor_copy(T.qf[:], T.qq[:]), "vs")
+    tiles = [(b, j, 4 * j + b) for b in range(4) for j in range(4)]
+    for w in ("V", "S", "P"):
+        wait(w, "vs", kq)
+        wait(w, "gs", gd)
+    vd, sd, pb = {}, {}, {}
+    for b, j, t in tiles:
+        vd[t] = did(V.tensor_scalar(T.dl[:, 128 * t:128 * t + 128], T.ident[:], T.qf[:, t:t + 1], None, A.mult), "vs")
+        sd[t] = did(S.activation(T.dh[:, 128 * t:128 * t + 128], T.ident[:], AF.Copy, scale=T.qf[:, 16 + t:17 + t]), "ss")
+    for b, j, t in tiles:
+        wait("P", "vs", vd[t])
+        wait("P", "ss", sd[t])
+        o = T["q%d" % b][:, 128 * j:128 * j + 128]
+        did(PE.matmul(o, T.ones[:], T.dl[:, 128 * t:128 * t + 128], True, False), "ps")
+        pb[b] = did(PE.matmul(o, T.o256[:], T.dh[:, 128 * t:128 * t + 128], False, True), "ps")
+    for t in range(NT):
+        did(V.tensor_scalar(T.mask[:, NH * t:NH * t + NH], T.iota12[:], T.qf[:, 32 + t:33 + t], None, A.is_equal), "vs")
+    p = 0
+    for b in range(4):
+        wait("V", "ps", pb[b])
+        u, bank = T.qu[:, 512 * b:512 * b + 512], T["q%d" % b][:]
+        ku = did(V.tensor_copy(u, bank), "vs")
+        wait("V", "vs", ku)
+        wait("S", "vs", ku)
+        ready = {}
+        for t in range(NV):
+            i = 512 * (b * NV + t)
+            ready[t] = ("vs", did(V.tensor_scalar(T.mv[:, i:i + 512], u, T.kf[:, t:t + 1], None, A.is_equal), "vs"))
+        for t in range(NV, NT):
+            i = 512 * (b * NS + t - NV)
+            a = did(S.activation(T.ma[:, i:i + 512], bank, AF.Abs, bias=T.kf[:, t:t + 1], scale=-1.0), "ss")
+            wait("S", "ss", a)
+            ready[t] = ("ss", did(S.activation(T.ms[:, i:i + 512], T.ma[:, i:i + 512], AF.Relu, bias=1.0, scale=-1.0), "ss"))
+        order = [0, 1, 2, 3, 13, 4, 5, 6, 7, 14, 8, 9, 10, 11, 12, 15]
+        for t in order:
+            wait("P", ready[t][0], ready[t][1])
+            for j in range(4):
+                o = T["r%d" % j][:, NH * b:NH * b + NH]
+                st, sp = t == order[0], t == order[-1]
+                if t < NV:
+                    i = 512 * (b * NV + t) + 128 * j
+                    p = did(PE.matmul(o, T.mv[:, i:i + 128], T.cls[:, NH * t:NH * t + NH], st, sp), "ps")
+                else:
+                    i, c = 512 * (b * NS + t - NV) + 128 * j, 2 * NH * (t - NV)
+                    did(PE.matmul(o, T.ms[:, i:i + 128], T.cs[:, c:c + NH], st, False), "ps")
+                    p = did(PE.matmul(o, T.ms[:, i:i + 128], T.cs[:, c + NH:c + 2 * NH], False, sp), "ps")
+    wait("V", "ps", p)
+    for j in range(4):
+        k = did(V.tensor_tensor(T.prod[:, 48 * j:48 * j + 48], T["r%d" % j][:, 0:48], T.mask[:, 48 * j:48 * j + 48], A.mult), "vs")
+    wait("V", "vs", k)
+    k = did(V.tensor_tensor(T.p1[:], T.prod[:, 0:192:2], T.prod[:, 1:192:2], A.add), "vs")
+    wait("V", "vs", k)
+    k = did(V.tensor_tensor(T.p2[:], T.p1[:, 0:96:2], T.p1[:, 1:96:2], A.add), "vs")
+    wait("V", "vs", k)
+    k = did(V.tensor_tensor(T.p3[:, 0:16], T.p2[:, 0:48:3], T.p2[:, 1:48:3], A.add), "vs")
+    wait("V", "vs", k)
+    k = did(V.tensor_tensor(T.p3[:, 16:32], T.p3[:, 0:16], T.p2[:, 2:48:3], A.add), "vs")
+    out = T.p3[:, 16:32]
+    if q:
+        wait("V", "vs", k)
+        k = did(V.tensor_scalar(T.p3[:, 32:48], out, 0.0, float(2048 * q), A.is_gt, A.mult), "vs")
+        wait("V", "vs", k)
+        k = did(V.tensor_tensor(T.p3[:, 48:64], out, T.p3[:, 32:48], A.add), "vs")
+        out = T.p3[:, 48:64]
+    dst, n = gat[(s, r)]
+    wait("g", "vs", k)
+    send([(out, T.codes[:, 64 * n + 16 * q:64 * n + 16 * q + 16], [dst], topo.mask(core, dst))], "cod%d" % n)

@@ -4,66 +4,68 @@ from concourse.mybir import dt, AluOpType, AxisListType, ActivationFunctionType
 A = AluOpType
 AF = ActivationFunctionType
 NR = 6
-NQ = 4
+NK = (22, 21, 21)
+ST = (0, 176, 344)
+NQT = 8
 NT = 16
-NS = 3
-NV = NT - NS
-NH = 12
+NS = 5
+NC = 36
 CAP = 512
 ZC = NR * CAP
 SL = 5
-NE = 4
+NP = 4
+PW = 8192 // NP
 
 SCRATCH = {
-    "qd": ("dram", [128, 16], "int32"),
-    "kd": ("dram", [128, 16], "int32"),
-    "kbs": ("dram", [4, 128, 16], "int32"),
-    "maps": ("dram", [6, 128, 16], "float32"),
-    "Qi": ("sbuf", [128, 16], "int32"),
-    "Ki": ("sbuf", [128, 16], "int32"),
-    "iota12": ("sbuf", [128, 12], "float32"),
-    "pI": ("sbuf", [128, 16], "int32"),
-    "pab": ("sbuf", [128, 32], "int32"),
-    "fab": ("sbuf", [128, 32], "float32"),
-    "cv": ("sbuf", [128, 80], "float32"),
+    "qh": ("dram", [256, 8], "int32"),
+    "ks0": ("dram", [128, 22], "int32"),
+    "ks1": ("dram", [128, 21], "int32"),
+    "ks2": ("dram", [128, 21], "int32"),
+    "maps": ("dram", [12, 128, 8], "float32"),
+    "Qi": ("sbuf", [128, 8], "int32"),
+    "Ki": ("sbuf", [128, 22], "int32"),
+    "iota36": ("sbuf", [128, NC], "float32"),
+    "pI": ("sbuf", [128, 22], "int32"),
+    "pab": ("sbuf", [128, 44], "int32"),
+    "fab": ("sbuf", [128, 44], "float32"),
+    "cv": ("sbuf", [128, 22 * 7], "float32"),
     "ones": ("sbuf", [128, 128], "bfloat16"),
     "o256": ("sbuf", [128, 128], "bfloat16"),
     "ident": ("sbuf", [128, 128], "bfloat16"),
-    "kk": ("sbuf", [128, 32], "int32"),
-    "kf": ("sbuf", [128, 32], "float32"),
-    "qq": ("sbuf", [128, 48], "int32"),
-    "qf": ("sbuf", [128, 48], "float32"),
-    "cls": ("sbuf", [128, NV * NH], "float16"),
-    "cs": ("sbuf", [128, 2 * NS * NH], "bfloat16"),
-    "dl": ("sbuf", [128, 2048], "bfloat16"),
-    "dh": ("sbuf", [128, 2048], "bfloat16"),
-    "qu": ("sbuf", [128, 2048], "uint16"),
-    "mv": ("sbuf", [128, 4 * NV * 512], "float16"),
-    "ma": ("sbuf", [128, 4 * NS * 512], "bfloat16"),
-    "ms": ("sbuf", [128, 4 * NS * 512], "bfloat16"),
-    "mask": ("sbuf", [128, 192], "float32"),
-    "prod": ("sbuf", [128, 192], "float32"),
-    "p1": ("sbuf", [128, 96], "float32"),
-    "p2": ("sbuf", [128, 48], "float32"),
-    "p3": ("sbuf", [128, 64], "float32"),
+    "kk": ("sbuf", [128, 44], "int32"),
+    "kf": ("sbuf", [128, 44], "float32"),
+    "qq": ("sbuf", [128, 24], "int32"),
+    "qf": ("sbuf", [128, 24], "float32"),
+    "zb": ("sbuf", [128, 17 * NC], "bfloat16"),
+    "cls": ("sbuf", [128, 17 * NC], "float16"),
+    "cs": ("sbuf", [128, NS * NC], "bfloat16"),
+    "dl": ("sbuf", [128, 1024], "bfloat16"),
+    "dh": ("sbuf", [128, 1024], "bfloat16"),
+    "qu": ("sbuf", [128, 1024], "uint16"),
+    "qs": ("sbuf", [128, 1024], "float32"),
+    "mv": ("sbuf", [128, 17 * 1024], "float16"),
+    "ma": ("sbuf", [128, NS * 1024], "bfloat16"),
+    "ms": ("sbuf", [128, NS * 1024], "bfloat16"),
+    "mask": ("sbuf", [128, NQT * NC], "float32"),
+    "prod": ("sbuf", [128, NQT * NC], "float32"),
+    "p1": ("sbuf", [128, 144], "float32"),
+    "p2": ("sbuf", [128, 72], "float32"),
+    "p3": ("sbuf", [128, 96], "float32"),
     "win": ("sbuf", [128, 8192], "bfloat16"),
-    "codes": ("sbuf", [128, 128], "float32"),
-    "nones": ("sbuf", [128, 128], "bfloat16"),
-    "m1": ("sbuf", [128, 128], "bfloat16"),
-    "zer": ("sbuf", [128, 16], "bfloat16"),
+    "codes": ("sbuf", [128, 96], "float32"),
+    "rep": ("sbuf", [128, 128], "float32"),
     "iota32": ("sbuf", [128, 32], "float32"),
     "iotap": ("sbuf", [128, 128], "float32"),
-    "h2": ("sbuf", [128, 64], "float32"),
     "G": ("sbuf", [128, 32], "float32"),
     "F": ("sbuf", [128, 32], "bfloat16"),
     "inc": ("sbuf", [128, 32], "bfloat16"),
     "si": ("sbuf", [128, 96], "int32"),
     "sf": ("sbuf", [128, 64], "float32"),
-    "c1": ("sbuf", [128, 32], "float32"),
     "smap": ("sbuf", [128, 32], "float32"),
-    "lh": ("sbuf", [128, 4096], "float32"),
-    "la2": ("sbuf", [128, 2 * SL * 128], "float32"),
+    "lh": ("sbuf", [128, 512], "float32"),
+    "la2": ("sbuf", [128, 2 * SL * 48], "float32"),
     "rh": ("sbuf", [128, 1024], "float32"),
+    "lsb": ("sbuf", [16, 64], "float32"),
     "off": ("sbuf", [128, 64], "uint16"),
     "gb": ("sbuf", [128, 1024], "bfloat16"),
     "ywin": ("sbuf", [128, ZC + 16], "bfloat16"),
@@ -71,11 +73,10 @@ SCRATCH = {
     "yoff": ("sbuf", [128, 128], "uint16"),
     "ysb": ("sbuf", [128, 2048], "bfloat16"),
 }
-for _i in range(4):
-    SCRATCH["q%d" % _i] = ("psum", [128, 512], "float32")
+for _i in range(8):
     SCRATCH["r%d" % _i] = ("psum", [128, 512], "float32")
-SEMAPHORES = ["la", "lb", "go", "t0", "t1", "fwd", "qar", "kar", "kl", "ql", "cod0", "cod1", "tabs", "map", "om",
-              "ml", "dat", "ls", "gs", "vs", "ss", "ps", "sy", "sa"]
+SEMAPHORES = ["la", "lb", "go", "t0", "t1", "t2", "t3", "b0", "b1", "b2", "b3", "fwd", "qar", "kar", "kl", "ql", "cod0",
+              "cod1", "map", "om", "ml", "dat", "ls", "gs", "vs", "ss", "ps", "sy", "sa"]
 
 
 def low_bits(mask, n, start=0):
@@ -83,26 +84,15 @@ def low_bits(mask, n, start=0):
     return sum(bits[start:start + n])
 
 
-def n_bits(mask):
-    return sum(mask >> i & 1 for i in range(16))
-
-
 def plan(T, topo, ncores=256):
     cores = list(T.cores)
-    chips = {}
-    where = {}
+    chips, where = {}, {}
     for c in range(ncores):
         where[c] = (topo.host(c), topo.chip(c))
         chips.setdefault(where[c], []).append(c)
-    used = set(where[c] for c in cores)
-    match, gat, jobs, helper = {}, {}, {}, {}
-    for s in range(NR):
-        near = [k for k in chips if k not in used and topo.same_plane(cores[s], chips[k][0])]
-        near.sort(key=lambda k: (k[0] != topo.host(cores[s]), abs(k[1] - topo.chip(cores[s])), k[1]))
-        for b, k in enumerate(near[:3]):
-            used.add(k)
-            for i in range(8):
-                match[(s, 2 * b + i // 4, i % 4)] = chips[k][i]
+    group = {s: [r for r in range(NR) if r == s or topo.same_plane(cores[s], cores[r])] for s in range(NR)}
+    big = max((group[s] for s in range(NR)), key=len)
+    gat, jobs, helper = {}, {}, {}
     for s in range(NR):
         c0 = cores[s]
         far = next(c for c in range(ncores) if topo.mates(c0, c))
@@ -111,20 +101,48 @@ def plan(T, topo, ncores=256):
         hb = next(c for c in port if topo.die(c) != topo.die(c0))
         helper[s] = (ha, hb)
         order = [(s + d) % NR for d in range(1, NR)]
-        sp = [r for r in order if topo.same_plane(c0, cores[r])]
-        rest = sp[1:] + [r for r in order if r not in sp]
+        sp = [r for r in order if r in group[s]]
+        rest = sp[1:] + [r for r in order if r not in group[s]]
         jobs[c0] = (s, [sp[0], s])
         jobs[ha] = (s, [rest[0], rest[2]])
         jobs[hb] = (s, [rest[1], rest[3]])
         for c in (c0, ha, hb):
             for n, r in enumerate(jobs[c][1]):
                 gat[(s, r)] = (c, n)
-    return cores, match, gat, jobs, helper
+    used = set(where[c] for c in cores)
+    inb, other = [], []
+    for k in chips:
+        if k not in used:
+            (inb if topo.same_plane(chips[k][0], cores[big[0]]) else other).extend(chips[k])
+    spare = [c for s in range(NR) if s not in big for c in chips[where[cores[s]]] if c != cores[s] and c not in helper[s]]
+    ports = [c for c in other if topo.may_write(c, cores[big[0]])]
+    match = {}
+
+    def give(pairs, pool):
+        for i, sr in enumerate(pairs):
+            match[sr] = pool[6 * i:6 * i + 6]
+        return pool[6 * len(pairs):]
+
+    every = [(s, r) for s in range(NR) for r in range(NR)]
+    give([p for p in every if p[0] in big and p[1] in big], inb)
+    left = give([p for p in every if p[0] in big and p[1] not in big], ports)
+    pool = [c for c in other if c not in ports or c in left] + spare
+    give([p for p in every if p[0] not in big], pool)
+    return cores, match, gat, jobs, helper, group
+
+
+def ask_direct(topo, cores, match, r, h):
+    return [match[(o, r)][3 * h + q] for o in range(NR) for q in range(3) if topo.may_write(cores[r], match[(o, r)][3 * h + q])]
+
+
+def parts(dests):
+    return [dests] if len(dests) <= 16 else [dests[:len(dests) // 2], dests[len(dests) // 2:]]
 
 
 def rank_program(g, core, T, topo):
-    cores, match, gat, jobs, helper = plan(T, topo)
-    role = next((key for key in match if match[key] == core), None)
+    P = plan(T, topo)
+    cores, match, gat, jobs, helper, group = P
+    role = next(((s, r, match[(s, r)].index(core)) for s, r in match if core in match[(s, r)]), None)
     if role is None and core not in jobs:
         return
     queues = {"g": g, "V": g.vector, "S": g.scalar, "P": g.tensor, "Y": g.sync}
@@ -144,285 +162,362 @@ def rank_program(g, core, T, topo):
         rid, pid = topo.addr(d, core)
         return DstId(rid=rid, pnc=pid)
 
+    def common(ds):
+        m = topo.mask(core, ds[0])
+        for d in ds:
+            m &= topo.mask(core, d)
+        return m
+
     def send(sets, sem):
-        g.remote_dma_fused([RemoteDMATransfer(dst_ids=[addr(d) for d in ds], dma_engine_mask=m, remote_sem=T.sem[sem],
-                                              srcs=[src], dsts=[dst for d in ds], alu_op=0)
-                            for src, dst, ds, m in sets], local_sem=T.sem.ls)
-        cnt["ls"] = cnt.get("ls", 0) + sum(n_bits(m) for src, dst, ds, m in sets)
+        every = [d for x in sets for d in x[2]]
+        m, at, tr = common(every), 0, []
+        for src, dst, ds, n in sets:
+            tr.append(RemoteDMATransfer(dst_ids=[addr(d) for d in ds], dma_engine_mask=low_bits(m, n, at),
+                                        remote_sem=T.sem[sem], srcs=[src], dsts=[dst for d in ds], alu_op=0))
+            at += n
+        g.remote_dma_fused(tr, local_sem=T.sem.ls)
+        cnt["ls"] = cnt.get("ls", 0) + at
 
     if role is not None:
-        run_match(g, core, T, topo, role, gat, did, wait, send)
+        run_match(g, core, T, topo, role, P, did, wait, send)
     else:
-        run_rank(g, core, T, topo, cores, match, gat, jobs, helper, did, wait, send)
+        run_rank(g, core, T, topo, P, did, wait, send)
     for sem in sorted(cnt):
         wait("g", sem, cnt[sem])
 
 
-def run_rank(g, core, T, topo, cores, match, gat, jobs, helper, did, wait, send):
+def run_rank(g, core, T, topo, P, did, wait, send):
+    cores, match, gat, jobs, helper, group = P
     V, S, PE, SY = g.vector, g.scalar, g.tensor, g.sync
     s, asked = jobs[core]
     is_rank = core == cores[s]
     ha, hb = helper[s]
-    did(g.iota(T.iota32[:], [[1, 32]], 0, 0, allow_small_or_imprecise_dtypes=True), "gs")
-    gi = did(g.iota(T.iotap[:], [[0, 8], [1, 16]], 0, 0, allow_small_or_imprecise_dtypes=True), "gs")
+    ks = [T.ks0, T.ks1, T.ks2]
+    nones, m1, zer = T.o256, T.ident, T.zb[:, 0:16]
+    crossing = [o for o in range(NR) if not topo.may_write(cores[s], match[(o, s)][0])]
+    if is_rank:
+        did(SY.dma_start(T.qh[:], T.ka[:]), "la", 16)
+        for q in range(3):
+            did(S.dma_start(ks[q][:], T.kb[:, ST[q]:ST[q] + 8 * NK[q]]), "lb", 16)
+    did(V.memset(nones[:], -1.0), "vs")
     did(V.memset(T.ones[:], 1.0), "vs")
-    did(V.memset(T.zer[:], 0.0), "vs")
-    vn = did(V.memset(T.nones[:], -1.0), "vs")
+    vn = did(V.memset(zer, 0.0), "vs")
     if is_rank:
         did(V.memset(T.ywin[:, ZC:ZC + 16], 0.0), "vs")
-        did(SY.dma_start(T.qd[:], T.ka[:]), "la", 16)
-        for q in range(NQ):
-            did(S.dma_start(T.kbs[q], T.kb[:, 128 * q:128 * q + 128]), "lb", 16)
+    did(g.iota(T.iota32[:], [[1, 32]], 0, 0, allow_small_or_imprecise_dtypes=True), "gs")
+    did(g.iota(T.iotap[:], [[0, 8], [1, 16]], 0, 0, allow_small_or_imprecise_dtypes=True), "gs")
+    gi = did(g.iota(T.pI[:, 0:2], [[0, 2]], 0, 1), "gs")
+    wait("g", "vs", vn)
+    gm = did(g.affine_select(m1[:], nones[:], [[-1, 128]], A.is_ge, 0.0, 0, 1), "gs")
+    wait("V", "gs", gi)
+    k = did(V.tensor_scalar(T.pab[:, 0:2], T.pI[:, 0:2], 15, None, A.bitwise_and), "vs")
+    wait("V", "vs", k)
+    k = did(V.tensor_copy(T.fab[:, 0:2], T.pab[:, 0:2]), "vs")
+    wait("V", "vs", k)
+    vrep = did(V.tensor_scalar(T.rep[:], T.iotap[:], T.fab[:, 0:1], None, A.is_equal), "vs")
+    if is_rank:
         wait("g", "la", 16)
-        on = topo.mask(core, ha)
-        send([(T.qd[:], T.qd[:], [ha, hb], low_bits(on, NE))], "fwd")
-        wait("g", "lb", 64)
-        off = topo.mask(core, match[(s, s, 0)])
-        send([(T.kbs[q], T.kd[:], [match[(s, r, q)] for r in range(NR)], low_bits(off, 2, 2 * q)) for q in range(NQ)], "kar")
-        near = [match[(o, s, q)] for o in range(NR) if topo.may_write(core, cores[o]) for q in range(NQ)]
-        send([(T.qd[:], T.qd[:], near, off)], "qar")
+        half = [T.qh[128 * h:128 * h + 128] for h in range(2)]
+        if crossing:
+            send([(half[h], half[h], [helper[s][h]], 2) for h in range(2)], "fwd")
+        sets = []
+        for h in range(2):
+            ps = parts(ask_direct(topo, cores, match, s, h))
+            sets += [(half[h], half[h], ds, 4 // len(ps)) for ds in ps]
+        send(sets, "qar")
+        wait("g", "lb", 48)
+        dk = [[ha, hb] + [match[(s, r)][3 * h + q] for r in group[s] for h in range(2)] for q in range(3)]
+        send([(ks[0][:], ks[0][:], dk[0], 8)], "kar")
+        send([(ks[q][:], ks[q][:], dk[q], 4) for q in (1, 2)], "kar")
         g.sem_inc(T.sem.go, 1)
         SY.wait_ge(T.sem.go, 1)
-        did(SY.dma_start(T.win[:, 0:4096], T.tab[:, 0:4096]), "t0", 16)
-        did(SY.dma_start(T.win[:, 4096:8192], T.tab[:, 4096:8192]), "t1", 16)
-        for h in range(2):
-            wait("g", "t%d" % h, 16)
-            w = T.win[:, 4096 * h:4096 * h + 4096]
-            send([(w, w, [ha, hb], on)], "tabs")
-        did(g.iota(T.pI[:], [[0, 16]], 0, 1), "gs")
-    wait("g", "vs", vn)
-    gm = did(g.affine_select(T.m1[:], T.nones[:], [[-1, 128]], A.is_ge, 0.0, 0, 1), "gs")
-    if is_rank:
-        wait("V", "gs", gm)
-        k = did(V.tensor_scalar(T.pab[:, 0:16], T.pI[:], 15, None, A.bitwise_and), "vs")
-        wait("V", "vs", k)
-        k = did(V.tensor_copy(T.fab[:, 0:16], T.pab[:, 0:16]), "vs")
-        wait("V", "vs", k)
-        rep = T.la2[:, 0:128] if False else T.cvrep[:] if False else T.mask[:, 0:128]
-        vrep = did(V.tensor_scalar(rep, T.iotap[:], T.fab[:, 0:1], None, A.is_equal), "vs")
+        for i in range(NP):
+            w = slice(PW * i, PW * i + PW)
+            did(SY.dma_start(T.win[:, w], T.tab[:, w]), "t%d" % i, 16)
+        for i in range(NP):
+            w = T.win[:, PW * i:PW * i + PW]
+            wait("g", "t%d" % i, 16)
+            send([(w, w, [ha], 16)], "b%d" % i)
     else:
         me = (ha, hb).index(core)
-        cross = [o for o in range(NR) if not topo.may_write(cores[s], cores[o])]
-        mine = cross[me * len(cross) // 2:(me + 1) * len(cross) // 2]
-        dsts = [match[(o, s, q)] for o in mine for q in range(NQ)]
-        wait("g", "fwd", NE)
-        send([(T.qd[:], T.qd[:], dsts, topo.mask(core, dsts[0]))], "qar")
-    wait("P", "gs", gm)
-    wait("P", "vs", vn)
-    wait("V", "gs", gm)
-    wait("S", "gs", gm)
+        if crossing:
+            wait("g", "fwd", 2)
+            half = T.qh[128 * me:128 * me + 128]
+            send([(half, half, [match[(o, s)][3 * me + q] for o in crossing for q in range(3)], 4)], "qar")
+        wait("g", "kar", 16)
+        dk = [[match[(s, r)][3 * me + q] for r in range(NR) if r not in group[s]] for q in range(3)]
+        send([(ks[0][:], ks[0][:], dk[0], 8)], "kar")
+        send([(ks[q][:], ks[q][:], dk[q], 4) for q in (1, 2)], "kar")
+        if core == ha:
+            for i in range(NP):
+                w = T.win[:, PW * i:PW * i + PW]
+                wait("g", "b%d" % i, 16)
+                send([(w, w, [hb], 16)], "b%d" % i)
+    for w in ("P", "V", "S"):
+        wait(w, "gs", gm)
+    wait("P", "vs", vrep)
     for n, r in enumerate(asked):
-        wait("V", "cod%d" % n, NQ * n_bits(topo.mask(match[(s, r, 0)], core)))
+        wait("V", "cod%d" % n, 6 * 8)
         c = 16 * n
-        G, F, inc, c1, sm = [t[:, c:c + 16] for t in (T.G, T.F, T.inc, T.c1, T.smap)]
-        h2 = T.h2[:, 32 * n:32 * n + 32]
-        k = did(V.tensor_tensor(h2, T.codes[:, 64 * n:64 * n + 32], T.codes[:, 64 * n + 32:64 * n + 64], A.add), "vs")
+        G, F, inc, sm = [t[:, c:c + 16] for t in (T.G, T.F, T.inc, T.smap)]
+        h2, c1 = T.p1[:, c:c + 16], T.p1[:, 32 + c:48 + c]
+        k = did(V.tensor_tensor(h2, T.codes[:, 48 * n:48 * n + 16], T.codes[:, 48 * n + 16:48 * n + 32], A.add), "vs")
         wait("V", "vs", k)
-        k = did(V.tensor_tensor(G, T.h2[:, 32 * n:32 * n + 16], T.h2[:, 32 * n + 16:32 * n + 32], A.add), "vs")
+        k = did(V.tensor_tensor(G, h2, T.codes[:, 48 * n + 32:48 * n + 48], A.add), "vs")
         wait("V", "vs", k)
         k = did(V.tensor_scalar(F, G, 0.0, None, A.is_gt), "vs")
         wait("V", "vs", k)
-        k = did(V.tensor_tensor_scan(inc, F, T.zer[:], 0.0, A.add, A.add), "vs")
+        k = did(V.tensor_tensor_scan(inc, F, zer, 0.0, A.add, A.add), "vs")
         wait("P", "vs", k)
-        slot = T["q%d" % n][:, 0:16]
-        did(PE.matmul(slot, T.m1[:], F, True, False), "ps")
+        did(V.tensor_scalar(T.p1[:, 64 + c:80 + c], G, -1.0, None, A.mult), "vs")
+        slot = T["r%d" % n][:, 0:16]
+        did(PE.matmul(slot, m1[:], F, True, False), "ps")
         p = did(PE.matmul(slot, T.ones[:], inc, False, True), "ps")
         wait("V", "ps", p)
         si = T.si[:, 48 * n:48 * n + 16]
         k1 = did(V.tensor_copy(si, slot), "vs")
-        k2 = did(V.tensor_scalar(c1, slot, float(CAP * s - ZC), None, A.add), "vs")
+        did(V.tensor_scalar(c1, slot, float(CAP * s - ZC), None, A.add), "vs")
         wait("V", "vs", k1)
         did(V.tensor_scalar(T.si[:, 48 * n + 16:48 * n + 32], si, 15, None, A.bitwise_and), "vs")
         k3 = did(V.tensor_scalar(T.si[:, 48 * n + 32:48 * n + 48], si, 4, None, A.arith_shift_right), "vs")
-        wait("V", "vs", k2)
-        km = did(V.tensor_tensor(sm, c1, F, A.mult), "vs")
         wait("V", "vs", k3)
         kf = did(V.tensor_copy(T.sf[:, 32 * n:32 * n + 32], T.si[:, 48 * n + 16:48 * n + 48]), "vs")
+        km = did(V.tensor_tensor(sm, c1, F, A.mult), "vs")
         wait("V", "vs", kf)
         if r == s:
             wait("Y", "vs", km)
-            did(SY.dma_start(T.maps[s], sm), "om", 16)
+            for h in range(2):
+                did(SY.dma_start(T.maps[2 * s + h], T.smap[:, c + 8 * h:c + 8 * h + 8]), "om", 16)
         else:
             wait("g", "vs", km)
-            send([(sm, T.maps[s], [cores[r]], topo.mask(core, cores[r]))], "map")
+            send([(T.smap[:, c + 8 * h:c + 8 * h + 8], T.maps[2 * s + h], [cores[r]], 4) for h in range(2)], "map")
         wait("S", "vs", kf)
-        lst = T["r%d" % n][:, 0:32]
+        lst = T["r%d" % (2 + n)][0:16, 0:32]
         tv, ts = {}, {}
         for t in range(NT):
             lo, hi = T.sf[:, 32 * n + t:32 * n + t + 1], T.sf[:, 32 * n + 16 + t:32 * n + 17 + t]
-            lh = T.lh[:, 2048 * n + 128 * t:2048 * n + 128 * t + 128]
+            lh = T.lh[:, 256 * n + 16 * t:256 * n + 16 * t + 16]
+            rh = T.rh[:, 512 * n + 32 * t:512 * n + 32 * t + 32]
             if t >= NT - SL:
-                i = (n * SL + t - NT + SL) * 128
-                a = did(S.activation(T.la2[:, i:i + 128], T.iotap[:], AF.Abs, bias=lo, scale=-1.0), "ss")
+                i = (n * SL + t - NT + SL) * 48
+                did(S.activation(T.la2[:, i:i + 16], T.iotap[:, 0:16], AF.Abs, bias=lo, scale=-1.0), "ss")
+                a = did(S.activation(T.la2[:, i + 16:i + 48], T.iota32[:], AF.Abs, bias=hi, scale=-1.0), "ss")
                 wait("S", "ss", a)
-                ts[t] = did(S.activation(lh, T.la2[:, i:i + 128], AF.Relu, bias=1.0, scale=-1.0), "ss")
+                did(S.activation(lh, T.la2[:, i:i + 16], AF.Relu, bias=1.0, scale=-1.0), "ss")
+                ts[t] = did(S.activation(rh, T.la2[:, i + 16:i + 48], AF.Relu, bias=T.G[:, c + t:c + t + 1],
+                                         scale=T.p1[:, 64 + c + t:65 + c + t]), "ss")
             else:
-                did(V.tensor_scalar(lh, T.iotap[:], lo, None, A.is_equal), "vs")
-            tv[t] = did(V.tensor_scalar(T.rh[:, 512 * n + 32 * t:512 * n + 32 * t + 32], T.iota32[:], hi,
-                                        T.G[:, c + t:c + t + 1], A.is_equal, A.mult), "vs")
+                did(V.tensor_scalar(lh, T.iotap[:, 0:16], lo, None, A.is_equal), "vs")
+                tv[t] = did(V.tensor_scalar(rh, T.iota32[:], hi, T.G[:, c + t:c + t + 1], A.is_equal, A.mult), "vs")
         for t in range(NT):
-            wait("P", "vs", tv[t])
             if t in ts:
                 wait("P", "ss", ts[t])
-            p = did(PE.matmul(lst, T.lh[:, 2048 * n + 128 * t:2048 * n + 128 * t + 128],
+            else:
+                wait("P", "vs", tv[t])
+            p = did(PE.matmul(lst, T.lh[:, 256 * n + 16 * t:256 * n + 16 * t + 16],
                               T.rh[:, 512 * n + 32 * t:512 * n + 32 * t + 32], t == 0, t == NT - 1), "ps")
         wait("V", "ps", p)
-        k = did(V.tensor_scalar(T.off[:, 32 * n:32 * n + 32], lst, -1.0, None, A.add), "vs")
+        lsb = T.lsb[:, 32 * n:32 * n + 32]
+        k = did(V.tensor_copy(lsb, lst), "vs")
+        wait("P", "vs", k)
+        lst8 = T["r%d" % (4 + n)][:, 0:32]
+        p = did(PE.matmul(lst8, T.rep[0:16, :], lsb, True, True), "ps")
+        wait("V", "ps", p)
+        k = did(V.tensor_scalar(T.off[:, 32 * n:32 * n + 32], lst8, -1.0, None, A.add), "vs")
         for q in ("V", "S"):
             wait(q, "vs", k)
-            if is_rank:
-                wait(q, "t0", 16)
-                wait(q, "t1", 16)
-            else:
-                wait(q, "tabs", 2 * n_bits(topo.mask(cores[s], core)))
+            for i in range(NP):
+                wait(q, "%s%d" % ("t" if is_rank else "b", i), 16)
         out = T.ywin if r == s else T.gb
         o = CAP * s if r == s else CAP * n
         kv = did(V.tensor_copy(out[:, o:o + 256], T.win[:, 0:8192].indirect(T.off[:, 32 * n:32 * n + 16])), "vs")
-        ks = did(S.activation(out[:, o + 256:o + 512], T.win[:, 0:8192].indirect(T.off[:, 32 * n + 16:32 * n + 32]), AF.Copy), "ss")
+        kc = did(S.activation(out[:, o + 256:o + 512], T.win[:, 0:8192].indirect(T.off[:, 32 * n + 16:32 * n + 32]), AF.Copy), "ss")
         if r != s:
             wait("g", "vs", kv)
-            wait("g", "ss", ks)
-            send([(T.gb[:, o:o + CAP], T.ywin[:, CAP * s:CAP * s + CAP], [cores[r]], topo.mask(core, cores[r]))], "dat")
+            wait("g", "ss", kc)
+            send([(T.gb[:, o:o + CAP], T.ywin[:, CAP * s:CAP * s + CAP], [cores[r]], 8)], "dat")
     if not is_rank:
         return
-    tot = sum(n_bits(topo.mask(gat[(o, s)][0], core)) for o in range(NR) if o != s)
+    tot = 8 * (NR - 1)
     wait("Y", "map", tot)
-    wait("Y", "om", 16)
+    wait("Y", "om", 32)
     did(SY.dma_start(T.msb[:], T.maps[:]), "ml", 16)
     wait("P", "ml", 16)
-    wait("P", "vs", vrep)
-    p = did(PE.matmul(T.q2[:, 0:128], T.mask[0:96, 0:128], T.msb[:], True, True), "ps")
+    p = did(PE.matmul(T.r6[:, 0:128], T.rep[0:96, :], T.msb[:], True, True), "ps")
     wait("V", "ps", p)
-    k = did(V.tensor_scalar(T.yoff[:], T.q2[:, 0:128], float(ZC), None, A.add), "vs")
+    k = did(V.tensor_scalar(T.yoff[:], T.r6[:, 0:128], float(ZC), None, A.add), "vs")
     for q in ("V", "S"):
         wait(q, "vs", k)
-        wait(q, "ss", ks)
+        wait(q, "ss", kc)
         wait(q, "dat", tot)
-    last = []
     for h in range(2):
-        a = 512 * h
-        k = did(V.tensor_copy(T.ysb[:, a:a + 512], T.ywin[:, 0:ZC + 16].indirect(T.yoff[:, 32 * h:32 * h + 32])), "vs")
-        wait("Y", "vs", k)
+        a, b = 512 * h, 1024 + 512 * h
+        kv = did(V.tensor_copy(T.ysb[:, a:a + 512], T.ywin[:, 0:ZC + 16].indirect(T.yoff[:, 32 * h:32 * h + 32])), "vs")
+        kc = did(S.activation(T.ysb[:, b:b + 512], T.ywin[:, 0:ZC + 16].indirect(T.yoff[:, 64 + 32 * h:96 + 32 * h]), AF.Copy), "ss")
+        wait("Y", "vs", kv)
         did(SY.dma_start(T.y[:, a:a + 512], T.ysb[:, a:a + 512]), "sy", 16)
-        b = 1024 + a
-        last.append(did(S.activation(T.ysb[:, b:b + 512], T.ywin[:, 0:ZC + 16].indirect(T.yoff[:, 64 + 32 * h:96 + 32 * h]), AF.Copy), "ss"))
-    for h in range(2):
-        b = 1024 + 512 * h
-        wait("S", "ss", last[h])
-        did(S.dma_start(T.y[:, b:b + 512], T.ysb[:, b:b + 512]), "sa", 16)
+        if h == 0:
+            wait("Y", "ss", kc)
+            did(SY.dma_start(T.y[:, b:b + 512], T.ysb[:, b:b + 512]), "sy", 16)
+        else:
+            wait("S", "ss", kc)
+            did(S.dma_start(T.y[:, b:b + 512], T.ysb[:, b:b + 512]), "sa", 16)
 
 
-def run_match(g, core, T, topo, role, gat, did, wait, send):
-    s, r, q = role
+def run_match(g, core, T, topo, role, P, did, wait, send):
+    cores, match, gat, jobs, helper, group = P
+    s, r, idx = role
+    q, h = idx % 3, idx // 3
+    n = NK[q]
+    nv = n - NS
     V, S, PE, SY = g.vector, g.scalar, g.tensor, g.sync
-    a256, v16, b1, val, tt = [T.cv[:, 16 * i:16 * i + 16] for i in range(5)]
-    did(g.iota(T.iota12[:], [[1, 12]], 0, 0, allow_small_or_imprecise_dtypes=True), "gs")
-    did(g.iota(T.pI[:], [[0, 16]], 0, 1), "gs")
-    gi = did(g.iota(tt, [[16, 16]], 0, 0, allow_small_or_imprecise_dtypes=True), "gs")
+    ks = [T.ks0, T.ks1, T.ks2][q]
+    C_HI, C_LO, C_CODE = 22, 44, 110
+    a16, hi16, b1, num, dbl, code, tt = [T.cv[:, 22 * i:22 * i + n] for i in range(7)]
+    direct = topo.may_write(cores[r], core)
+    wait("S", "qar", 4 // len(parts(ask_direct(topo, cores, match, r, h))) if direct else 4)
+    did(S.dma_start(T.Qi[:], T.qh[128 * h:128 * h + 128]), "ql", 16)
+    wait("Y", "kar", 4 if q else 8)
+    did(SY.dma_start(T.Ki[:, 0:n], ks[:]), "kl", 16)
+    did(g.iota(T.pI[:, 0:n], [[0, n]], 0, 1), "gs")
+    gi = did(g.iota(tt, [[16, n]], 0, 0, allow_small_or_imprecise_dtypes=True), "gs")
+    did(g.iota(T.iota36[:], [[1, 12], [0, 3]], 0, 0, allow_small_or_imprecise_dtypes=True), "gs")
     k = did(V.memset(T.ones[:], 1.0), "vs")
     did(V.memset(T.o256[:], 256.0), "vs")
+    kz = did(V.memset(T.zb[:], 0.0), "vs")
+    did(V.memset(T.cs[:], 0.0), "vs")
     wait("g", "vs", k)
     gd = did(g.affine_select(T.ident[:], T.ones[:], [[-1, 128]], A.is_equal, 0.0, 0, 1), "gs")
+    wait("V", "vs", kz)
+    did(V.tensor_copy(T.cls[:], T.zb[:]), "vs")
     wait("V", "gs", gi)
-    did(V.tensor_scalar(T.pab[:, 0:16], T.pI[:], 7, None, A.bitwise_and), "vs")
-    k = did(V.tensor_scalar(T.pab[:, 16:32], T.pI[:], 3, None, A.arith_shift_right), "vs")
+    did(V.tensor_scalar(T.pab[:, 0:n], T.pI[:, 0:n], 7, None, A.bitwise_and), "vs")
+    k = did(V.tensor_scalar(T.pab[:, 22:22 + n], T.pI[:, 0:n], 3, None, A.arith_shift_right), "vs")
     wait("V", "vs", k)
-    k = did(V.tensor_copy(T.fab[:], T.pab[:]), "vs")
+    did(V.tensor_copy(T.fab[:, 0:n], T.pab[:, 0:n]), "vs")
+    k = did(V.tensor_copy(T.fab[:, 22:22 + n], T.pab[:, 22:22 + n]), "vs")
     wait("V", "vs", k)
-    did(V.tensor_scalar(a256, T.fab[:, 0:16], 256.0, None, A.mult), "vs")
-    k = did(V.tensor_scalar(b1, T.fab[:, 16:32], 1.0, None, A.add), "vs")
+    did(V.tensor_scalar(a16, T.fab[:, 0:n], float(16 * n), None, A.mult), "vs")
+    k = did(V.tensor_scalar(b1, T.fab[:, 22:22 + n], 1.0, None, A.add), "vs")
     wait("V", "vs", k)
-    k = did(V.tensor_tensor(v16, a256, tt, A.add), "vs")
+    k = did(V.tensor_tensor(hi16, a16, tt, A.add), "vs")
     wait("V", "vs", k)
-    k = did(V.tensor_tensor(val, v16, b1, A.add), "vs")
+    k = did(V.tensor_tensor(num, hi16, b1, A.add), "vs")
     wait("V", "vs", k)
-    wait("Y", "kar", 2)
-    did(SY.dma_start(T.Ki[:], T.kd[:]), "kl", 16)
-    wait("S", "qar", n_bits(topo.mask(T.cores[s], core)))
-    did(S.dma_start(T.Qi[:], T.qd[:]), "ql", 16)
-    wait("V", "kl", 16)
-    did(V.tensor_scalar(T.kk[:, 0:16], T.Ki[:], 65535, None, A.bitwise_and), "vs")
-    k = did(V.tensor_scalar(T.kk[:, 16:32], T.Ki[:], 16, None, A.arith_shift_right), "vs")
+    k = did(V.tensor_scalar(dbl, num, 2.0, -2048.0, A.mult, A.add), "vs")
     wait("V", "vs", k)
-    k = did(V.tensor_copy(T.kf[:], T.kk[:]), "vs")
+    k = did(V.tensor_tensor(code, num, dbl, A.max), "vs")
     wait("V", "vs", k)
-    for t in range(NT):
-        hi = T.kf[:, 16 + t:17 + t]
-        if t < NV:
-            did(V.tensor_scalar(T.cls[:, NH * t:NH * t + NH], T.iota12[:], hi, T.cv[:, 48 + t:49 + t], A.is_equal, A.mult), "vs")
-        else:
-            i = 2 * NH * (t - NV)
-            did(V.tensor_scalar(T.cs[:, i:i + NH], T.iota12[:], hi, T.cv[:, 16 + t:17 + t], A.is_equal, A.mult), "vs")
-            did(V.tensor_scalar(T.cs[:, i + NH:i + 2 * NH], T.iota12[:], hi, T.cv[:, 32 + t:33 + t], A.is_equal, A.mult), "vs")
-    wait("V", "ql", 16)
-    did(V.tensor_scalar(T.qq[:, 0:16], T.Qi[:], 255, None, A.bitwise_and), "vs")
-    did(V.tensor_scalar(T.qq[:, 16:32], T.Qi[:], 8, 255, A.arith_shift_right, A.bitwise_and), "vs")
-    k = did(V.tensor_scalar(T.qq[:, 32:48], T.Qi[:], 16, None, A.arith_shift_right), "vs")
-    wait("V", "vs", k)
-    kq = did(V.tensor_copy(T.qf[:], T.qq[:]), "vs")
-    tiles = [(b, j, 4 * j + b) for b in range(4) for j in range(4)]
     for w in ("V", "S", "P"):
-        wait(w, "vs", kq)
         wait(w, "gs", gd)
-    vd, sd, pb = {}, {}, {}
-    for b, j, t in tiles:
-        vd[t] = did(V.tensor_scalar(T.dl[:, 128 * t:128 * t + 128], T.ident[:], T.qf[:, t:t + 1], None, A.mult), "vs")
-        sd[t] = did(S.activation(T.dh[:, 128 * t:128 * t + 128], T.ident[:], AF.Copy, scale=T.qf[:, 16 + t:17 + t]), "ss")
-    for b, j, t in tiles:
-        wait("P", "vs", vd[t])
-        wait("P", "ss", sd[t])
-        o = T["q%d" % b][:, 128 * j:128 * j + 128]
-        did(PE.matmul(o, T.ones[:], T.dl[:, 128 * t:128 * t + 128], True, False), "ps")
-        pb[b] = did(PE.matmul(o, T.o256[:], T.dh[:, 128 * t:128 * t + 128], False, True), "ps")
-    for t in range(NT):
-        did(V.tensor_scalar(T.mask[:, NH * t:NH * t + NH], T.iota12[:], T.qf[:, 32 + t:33 + t], None, A.is_equal), "vs")
-    p = 0
-    for b in range(4):
+    wait("V", "ql", 16)
+    did(V.tensor_scalar(T.qq[:, 0:8], T.Qi[:], 255, None, A.bitwise_and), "vs")
+    did(V.tensor_scalar(T.qq[:, 8:16], T.Qi[:], 8, 255, A.arith_shift_right, A.bitwise_and), "vs")
+    k = did(V.tensor_scalar(T.qq[:, 16:24], T.Qi[:], 16, None, A.arith_shift_right), "vs")
+    wait("V", "vs", k)
+    k = did(V.tensor_copy(T.qf[:], T.qq[:]), "vs")
+    for w in ("V", "S", "P"):
+        wait(w, "vs", k)
+    vd, sd = {}, {}
+    for j in range(NQT):
+        vd[j] = did(V.tensor_scalar(T.dl[:, 128 * j:128 * j + 128], T.ident[:], T.qf[:, j:j + 1], None, A.mult), "vs")
+        sd[j] = did(S.activation(T.dh[:, 128 * j:128 * j + 128], T.ident[:], AF.Copy, scale=T.qf[:, 8 + j:9 + j]), "ss")
+    pb = {}
+    for b in range(2):
+        bank = T["r%d" % (6 + b)][:]
+        wait("P", "vs", vd[4 * b + 3])
+        did(PE.matmul(bank, T.ones[:], T.dl[:, 512 * b:512 * b + 512], True, False), "ps")
+        wait("P", "ss", sd[4 * b + 3])
+        pb[b] = did(PE.matmul(bank, T.o256[:], T.dh[:, 512 * b:512 * b + 512], False, True), "ps")
+    wait("V", "kl", 16)
+    did(V.tensor_scalar(T.kk[:, 0:n], T.Ki[:, 0:n], 65535, None, A.bitwise_and), "vs")
+    k = did(V.tensor_scalar(T.kk[:, 22:22 + n], T.Ki[:, 0:n], 16, None, A.arith_shift_right), "vs")
+    wait("V", "vs", k)
+    did(V.tensor_copy(T.kf[:, 0:n], T.kk[:, 0:n]), "vs")
+    k = did(V.tensor_copy(T.kf[:, 22:22 + n], T.kk[:, 22:22 + n]), "vs")
+    wait("V", "vs", k)
+    iota12 = T.iota36[:, 0:NC:3]
+    cl = {}
+
+    def classes(t):
+        hi = T.kf[:, 22 + t:23 + t]
+        if t < nv:
+            o = NC * t
+            cl[t] = did(V.tensor_scalar(T.cls[:, o:o + NC:3], iota12, hi, T.cv[:, C_CODE + t:C_CODE + t + 1], A.is_equal, A.mult), "vs")
+        else:
+            o = NC * (t - nv)
+            did(V.tensor_scalar(T.cs[:, o + 1:o + NC:3], iota12, hi, T.cv[:, C_HI + t:C_HI + t + 1], A.is_equal, A.mult), "vs")
+            cl[t] = did(V.tensor_scalar(T.cs[:, o + 2:o + NC:3], iota12, hi, T.cv[:, C_LO + t:C_LO + t + 1], A.is_equal, A.mult), "vs")
+
+    order = list(range(nv))
+    for k, at in enumerate((5, 10, 15, nv + 2, nv + 4)):
+        order.insert(at, nv + k)
+    early, late = order[:9], order[9:]
+    for t in early:
+        classes(t)
+    sc = {}
+    for b in range(2):
+        bank = T["r%d" % (6 + b)][:]
         wait("V", "ps", pb[b])
-        u, bank = T.qu[:, 512 * b:512 * b + 512], T["q%d" % b][:]
-        ku = did(V.tensor_copy(u, bank), "vs")
-        wait("V", "vs", ku)
+        ku = did(V.tensor_copy(T.qu[:, 512 * b:512 * b + 512], bank), "vs")
         wait("S", "vs", ku)
-        ready = {}
-        for t in range(NV):
-            i = 512 * (b * NV + t)
-            ready[t] = ("vs", did(V.tensor_scalar(T.mv[:, i:i + 512], u, T.kf[:, t:t + 1], None, A.is_equal), "vs"))
-        for t in range(NV, NT):
-            i = 512 * (b * NS + t - NV)
-            a = did(S.activation(T.ma[:, i:i + 512], bank, AF.Abs, bias=T.kf[:, t:t + 1], scale=-1.0), "ss")
-            wait("S", "ss", a)
-            ready[t] = ("ss", did(S.activation(T.ms[:, i:i + 512], T.ma[:, i:i + 512], AF.Relu, bias=1.0, scale=-1.0), "ss"))
-        order = [0, 1, 2, 3, 13, 4, 5, 6, 7, 14, 8, 9, 10, 11, 12, 15]
-        for t in order:
-            wait("P", ready[t][0], ready[t][1])
-            for j in range(4):
-                o = T["r%d" % j][:, NH * b:NH * b + NH]
-                st, sp = t == order[0], t == order[-1]
-                if t < NV:
-                    i = 512 * (b * NV + t) + 128 * j
-                    p = did(PE.matmul(o, T.mv[:, i:i + 128], T.cls[:, NH * t:NH * t + NH], st, sp), "ps")
-                else:
-                    i, c = 512 * (b * NS + t - NV) + 128 * j, 2 * NH * (t - NV)
-                    did(PE.matmul(o, T.ms[:, i:i + 128], T.cs[:, c:c + NH], st, False), "ps")
-                    p = did(PE.matmul(o, T.ms[:, i:i + 128], T.cs[:, c + NH:c + 2 * NH], False, sp), "ps")
-    wait("V", "ps", p)
-    for j in range(4):
-        k = did(V.tensor_tensor(T.prod[:, 48 * j:48 * j + 48], T["r%d" % j][:, 0:48], T.mask[:, 48 * j:48 * j + 48], A.mult), "vs")
+        sc[b] = did(S.activation(T.qs[:, 512 * b:512 * b + 512], bank, AF.Copy), "ss")
+    wait("V", "vs", ku)
+    wait("S", "ss", sc[1])
+    ready = {}
+    for t in range(nv):
+        ready[t] = ("vs", did(V.tensor_scalar(T.mv[:, 1024 * t:1024 * t + 1024], T.qu[:], T.kf[:, t:t + 1], None, A.is_equal), "vs"))
+        for x in late[t:t + 1]:
+            classes(x)
+    for t in range(nv, n):
+        i = 1024 * (t - nv)
+        a = did(S.activation(T.ma[:, i:i + 1024], T.qs[:], AF.Abs, bias=T.kf[:, t:t + 1], scale=-1.0), "ss")
+        wait("S", "ss", a)
+        ready[t] = ("ss", did(S.activation(T.ms[:, i:i + 1024], T.ma[:, i:i + 1024], AF.Relu, bias=1.0, scale=-1.0), "ss"))
+    for j in range(NQT):
+        km = did(V.tensor_scalar(T.mask[:, NC * j:NC * j + NC], T.iota36[:], T.qf[:, 16 + j:17 + j], None, A.is_equal), "vs")
+    for t in order:
+        wait("P", ready[t][0], ready[t][1])
+        wait("P", "vs", cl[t])
+        for j in range(NQT):
+            if j >= 6:
+                wait("P", "ss", sc[j - 6])
+            o = T["r%d" % j][:, 0:NC]
+            if t < nv:
+                lhs, rhs = T.mv[:, 1024 * t + 128 * j:1024 * t + 128 * j + 128], T.cls[:, NC * t:NC * t + NC]
+            else:
+                i = t - nv
+                lhs, rhs = T.ms[:, 1024 * i + 128 * j:1024 * i + 128 * j + 128], T.cs[:, NC * i:NC * i + NC]
+            p = did(PE.matmul(o, lhs, rhs, t == order[0], t == order[-1]), "ps")
+    wait("V", "vs", km)
+    for j in range(NQT):
+        wait("V", "ps", p - NQT + 1 + j)
+        k = did(V.tensor_tensor(T.prod[:, j:NQT * NC:NQT], T["r%d" % j][:, 0:NC], T.mask[:, NC * j:NC * j + NC], A.mult), "vs")
     wait("V", "vs", k)
-    k = did(V.tensor_tensor(T.p1[:], T.prod[:, 0:192:2], T.prod[:, 1:192:2], A.add), "vs")
+    k = did(V.tensor_tensor(T.p1[:], T.prod[:, 0:144], T.prod[:, 144:288], A.add), "vs")
     wait("V", "vs", k)
-    k = did(V.tensor_tensor(T.p2[:], T.p1[:, 0:96:2], T.p1[:, 1:96:2], A.add), "vs")
+    k = did(V.tensor_tensor(T.p2[:], T.p1[:, 0:72], T.p1[:, 72:144], A.add), "vs")
     wait("V", "vs", k)
-    k = did(V.tensor_tensor(T.p3[:, 0:16], T.p2[:, 0:48:3], T.p2[:, 1:48:3], A.add), "vs")
+    k = did(V.tensor_tensor(T.p3[:, 0:24], T.p2[:, 0:24], T.p2[:, 24:48], A.add), "vs")
     wait("V", "vs", k)
-    k = did(V.tensor_tensor(T.p3[:, 16:32], T.p3[:, 0:16], T.p2[:, 2:48:3], A.add), "vs")
-    out = T.p3[:, 16:32]
+    k = did(V.tensor_tensor(T.p3[:, 24:48], T.p3[:, 0:24], T.p2[:, 48:72], A.add), "vs")
+    wait("V", "vs", k)
+    v, w, f, m, x, y = [T.p3[:, 48 + 8 * i:56 + 8 * i] for i in range(6)]
+    num_v = T.p3[:, 24:32]
+    did(V.tensor_scalar(w, num_v, 0.5, 1024.0, A.mult, A.add), "vs")
+    k = did(V.tensor_tensor(f, T.p3[:, 32:40], T.p3[:, 40:48], A.add), "vs")
+    wait("V", "vs", k)
+    k = did(V.tensor_tensor(m, num_v, w, A.min), "vs")
+    wait("V", "vs", k)
+    k = did(V.tensor_tensor(x, m, f, A.add), "vs")
+    out = x
     if q:
         wait("V", "vs", k)
-        k = did(V.tensor_scalar(T.p3[:, 32:48], out, 0.0, float(2048 * q), A.is_gt, A.mult), "vs")
+        k = did(V.tensor_scalar(v, x, 0.0, float(16 * ST[q]), A.is_gt, A.mult), "vs")
         wait("V", "vs", k)
-        k = did(V.tensor_tensor(T.p3[:, 48:64], out, T.p3[:, 32:48], A.add), "vs")
-        out = T.p3[:, 48:64]
-    dst, n = gat[(s, r)]
+        k = did(V.tensor_tensor(y, x, v, A.add), "vs")
+        out = y
+    dst, nth = gat[(s, r)]
     wait("g", "vs", k)
-    send([(out, T.codes[:, 64 * n + 16 * q:64 * n + 16 * q + 16], [dst], topo.mask(core, dst))], "cod%d" % n)
+    o = 48 * nth + 16 * q + 8 * h
+    send([(out, T.codes[:, o:o + 8], [dst], 8)], "cod%d" % nth)

from concourse.bass import DstId, RemoteDMATransfer
from concourse.mybir import dt, AluOpType, AxisListType, ActivationFunctionType

A = AluOpType
AF = ActivationFunctionType
NR = 6
NK = (22, 21, 21)
ST = (0, 176, 344)
NQT = 8
NT = 16
NS = 5
NC = 36
CAP = 512
ZC = NR * CAP
SL = 5
NP = 4
PW = 8192 // NP

SCRATCH = {
    "qh": ("dram", [256, 8], "int32"),
    "ks0": ("dram", [128, 22], "int32"),
    "ks1": ("dram", [128, 21], "int32"),
    "ks2": ("dram", [128, 21], "int32"),
    "maps": ("dram", [12, 128, 8], "float32"),
    "Qi": ("sbuf", [128, 8], "int32"),
    "Ki": ("sbuf", [128, 22], "int32"),
    "iota36": ("sbuf", [128, NC], "float32"),
    "pI": ("sbuf", [128, 22], "int32"),
    "pab": ("sbuf", [128, 44], "int32"),
    "fab": ("sbuf", [128, 44], "float32"),
    "cv": ("sbuf", [128, 22 * 7], "float32"),
    "ones": ("sbuf", [128, 128], "bfloat16"),
    "o256": ("sbuf", [128, 128], "bfloat16"),
    "ident": ("sbuf", [128, 128], "bfloat16"),
    "kk": ("sbuf", [128, 44], "int32"),
    "kf": ("sbuf", [128, 44], "float32"),
    "qq": ("sbuf", [128, 24], "int32"),
    "qf": ("sbuf", [128, 24], "float32"),
    "zb": ("sbuf", [128, 17 * NC], "bfloat16"),
    "cls": ("sbuf", [128, 17 * NC], "float16"),
    "cs": ("sbuf", [128, NS * NC], "bfloat16"),
    "dl": ("sbuf", [128, 1024], "bfloat16"),
    "dh": ("sbuf", [128, 1024], "bfloat16"),
    "qu": ("sbuf", [128, 1024], "uint16"),
    "qs": ("sbuf", [128, 1024], "float32"),
    "mv": ("sbuf", [128, 17 * 1024], "float16"),
    "ma": ("sbuf", [128, NS * 1024], "bfloat16"),
    "ms": ("sbuf", [128, NS * 1024], "bfloat16"),
    "mask": ("sbuf", [128, NQT * NC], "float32"),
    "prod": ("sbuf", [128, NQT * NC], "float32"),
    "p1": ("sbuf", [128, 144], "float32"),
    "p2": ("sbuf", [128, 72], "float32"),
    "p3": ("sbuf", [128, 96], "float32"),
    "win": ("sbuf", [128, 8192], "bfloat16"),
    "codes": ("sbuf", [128, 96], "float32"),
    "rep": ("sbuf", [128, 128], "float32"),
    "iota32": ("sbuf", [128, 32], "float32"),
    "iotap": ("sbuf", [128, 128], "float32"),
    "G": ("sbuf", [128, 32], "float32"),
    "F": ("sbuf", [128, 32], "bfloat16"),
    "inc": ("sbuf", [128, 32], "bfloat16"),
    "si": ("sbuf", [128, 96], "int32"),
    "sf": ("sbuf", [128, 64], "float32"),
    "smap": ("sbuf", [128, 32], "float32"),
    "lh": ("sbuf", [128, 512], "float32"),
    "la2": ("sbuf", [128, 2 * SL * 48], "float32"),
    "rh": ("sbuf", [128, 1024], "float32"),
    "lsb": ("sbuf", [16, 64], "float32"),
    "off": ("sbuf", [128, 64], "uint16"),
    "gb": ("sbuf", [128, 1024], "bfloat16"),
    "ywin": ("sbuf", [128, ZC + 16], "bfloat16"),
    "msb": ("sbuf", [96, 128], "float32"),
    "yoff": ("sbuf", [128, 128], "uint16"),
    "ysb": ("sbuf", [128, 2048], "bfloat16"),
}
for _i in range(8):
    SCRATCH["r%d" % _i] = ("psum", [128, 512], "float32")
SEMAPHORES = ["la", "lb", "go", "t0", "t1", "t2", "t3", "b0", "b1", "b2", "b3", "fwd", "qar", "kar", "kl", "ql", "cod0",
              "cod1", "map", "om", "ml", "dat", "ls", "gs", "vs", "ss", "ps", "sy", "sa"]


def low_bits(mask, n, start=0):
    bits = [1 << i for i in range(16) if mask >> i & 1]
    return sum(bits[start:start + n])


def plan(T, topo, ncores=256):
    cores = list(T.cores)
    chips, where = {}, {}
    for c in range(ncores):
        where[c] = (topo.host(c), topo.chip(c))
        chips.setdefault(where[c], []).append(c)
    group = {s: [r for r in range(NR) if r == s or topo.same_plane(cores[s], cores[r])] for s in range(NR)}
    big = max((group[s] for s in range(NR)), key=len)
    gat, jobs, helper = {}, {}, {}
    for s in range(NR):
        c0 = cores[s]
        far = next(c for c in range(ncores) if topo.mates(c0, c))
        port = [c for c in chips[where[c0]] if c != c0 and topo.may_write(c, far)]
        ha = next(c for c in port if topo.die(c) == topo.die(c0))
        hb = next(c for c in port if topo.die(c) != topo.die(c0))
        helper[s] = (ha, hb)
        order = [(s + d) % NR for d in range(1, NR)]
        sp = [r for r in order if r in group[s]]
        rest = sp[1:] + [r for r in order if r not in group[s]]
        jobs[c0] = (s, [sp[0], s])
        jobs[ha] = (s, [rest[0], rest[2]])
        jobs[hb] = (s, [rest[1], rest[3]])
        for c in (c0, ha, hb):
            for n, r in enumerate(jobs[c][1]):
                gat[(s, r)] = (c, n)
    used = set(where[c] for c in cores)
    inb, other = [], []
    for k in chips:
        if k not in used:
            (inb if topo.same_plane(chips[k][0], cores[big[0]]) else other).extend(chips[k])
    spare = [c for s in range(NR) if s not in big for c in chips[where[cores[s]]] if c != cores[s] and c not in helper[s]]
    ports = [c for c in other if topo.may_write(c, cores[big[0]])]
    match = {}

    def give(pairs, pool):
        for i, sr in enumerate(pairs):
            match[sr] = pool[6 * i:6 * i + 6]
        return pool[6 * len(pairs):]

    every = [(s, r) for s in range(NR) for r in range(NR)]
    give([p for p in every if p[0] in big and p[1] in big], inb)
    left = give([p for p in every if p[0] in big and p[1] not in big], ports)
    pool = [c for c in other if c not in ports or c in left] + spare
    give([p for p in every if p[0] not in big], pool)
    return cores, match, gat, jobs, helper, group


def ask_direct(topo, cores, match, r, h):
    return [match[(o, r)][3 * h + q] for o in range(NR) for q in range(3) if topo.may_write(cores[r], match[(o, r)][3 * h + q])]


def parts(dests):
    return [dests] if len(dests) <= 16 else [dests[:len(dests) // 2], dests[len(dests) // 2:]]


def rank_program(g, core, T, topo):
    P = plan(T, topo)
    cores, match, gat, jobs, helper, group = P
    role = next(((s, r, match[(s, r)].index(core)) for s, r in match if core in match[(s, r)]), None)
    if role is None and core not in jobs:
        return
    queues = {"g": g, "V": g.vector, "S": g.scalar, "P": g.tensor, "Y": g.sync}
    cnt, seen = {}, {}

    def did(inst, sem, n=1):
        inst.then_inc(T.sem[sem], n)
        cnt[sem] = cnt.get(sem, 0) + n
        return cnt[sem]

    def wait(q, sem, n):
        if seen.get((q, sem), 0) < n:
            seen[(q, sem)] = n
            queues[q].wait_ge(T.sem[sem], n)

    def addr(d):
        rid, pid = topo.addr(d, core)
        return DstId(rid=rid, pnc=pid)

    def common(ds):
        m = topo.mask(core, ds[0])
        for d in ds:
            m &= topo.mask(core, d)
        return m

    def send(sets, sem):
        every = [d for x in sets for d in x[2]]
        m, at, tr = common(every), 0, []
        for src, dst, ds, n in sets:
            tr.append(RemoteDMATransfer(dst_ids=[addr(d) for d in ds], dma_engine_mask=low_bits(m, n, at),
                                        remote_sem=T.sem[sem], srcs=[src], dsts=[dst for d in ds], alu_op=0))
            at += n
        g.remote_dma_fused(tr, local_sem=T.sem.ls)
        cnt["ls"] = cnt.get("ls", 0) + at

    if role is not None:
        run_match(g, core, T, topo, role, P, did, wait, send)
    else:
        run_rank(g, core, T, topo, P, did, wait, send)
    for sem in sorted(cnt):
        wait("g", sem, cnt[sem])


def run_rank(g, core, T, topo, P, did, wait, send):
    cores, match, gat, jobs, helper, group = P
    V, S, PE, SY = g.vector, g.scalar, g.tensor, g.sync
    s, asked = jobs[core]
    is_rank = core == cores[s]
    ha, hb = helper[s]
    ks = [T.ks0, T.ks1, T.ks2]
    nones, m1, zer = T.o256, T.ident, T.zb[:, 0:16]
    crossing = [o for o in range(NR) if not topo.may_write(cores[s], match[(o, s)][0])]
    if is_rank:
        did(SY.dma_start(T.qh[:], T.ka[:]), "la", 16)
        for q in range(3):
            did(S.dma_start(ks[q][:], T.kb[:, ST[q]:ST[q] + 8 * NK[q]]), "lb", 16)
    did(V.memset(nones[:], -1.0), "vs")
    did(V.memset(T.ones[:], 1.0), "vs")
    vn = did(V.memset(zer, 0.0), "vs")
    if is_rank:
        did(V.memset(T.ywin[:, ZC:ZC + 16], 0.0), "vs")
    did(g.iota(T.iota32[:], [[1, 32]], 0, 0, allow_small_or_imprecise_dtypes=True), "gs")
    did(g.iota(T.iotap[:], [[0, 8], [1, 16]], 0, 0, allow_small_or_imprecise_dtypes=True), "gs")
    gi = did(g.iota(T.pI[:, 0:2], [[0, 2]], 0, 1), "gs")
    wait("g", "vs", vn)
    gm = did(g.affine_select(m1[:], nones[:], [[-1, 128]], A.is_ge, 0.0, 0, 1), "gs")
    wait("V", "gs", gi)
    k = did(V.tensor_scalar(T.pab[:, 0:2], T.pI[:, 0:2], 15, None, A.bitwise_and), "vs")
    wait("V", "vs", k)
    k = did(V.tensor_copy(T.fab[:, 0:2], T.pab[:, 0:2]), "vs")
    wait("V", "vs", k)
    vrep = did(V.tensor_scalar(T.rep[:], T.iotap[:], T.fab[:, 0:1], None, A.is_equal), "vs")
    if is_rank:
        wait("g", "la", 16)
        half = [T.qh[128 * h:128 * h + 128] for h in range(2)]
        if crossing:
            send([(half[h], half[h], [helper[s][h]], 2) for h in range(2)], "fwd")
        sets = []
        for h in range(2):
            ps = parts(ask_direct(topo, cores, match, s, h))
            sets += [(half[h], half[h], ds, 4 // len(ps)) for ds in ps]
        send(sets, "qar")
        wait("g", "lb", 48)
        dk = [[ha, hb] + [match[(s, r)][3 * h + q] for r in group[s] for h in range(2)] for q in range(3)]
        send([(ks[0][:], ks[0][:], dk[0], 8)], "kar")
        send([(ks[q][:], ks[q][:], dk[q], 4) for q in (1, 2)], "kar")
        g.sem_inc(T.sem.go, 1)
        SY.wait_ge(T.sem.go, 1)
        for i in range(NP):
            w = slice(PW * i, PW * i + PW)
            did(SY.dma_start(T.win[:, w], T.tab[:, w]), "t%d" % i, 16)
        for i in range(NP):
            w = T.win[:, PW * i:PW * i + PW]
            wait("g", "t%d" % i, 16)
            send([(w, w, [ha], 16)], "b%d" % i)
    else:
        me = (ha, hb).index(core)
        if crossing:
            wait("g", "fwd", 2)
            half = T.qh[128 * me:128 * me + 128]
            send([(half, half, [match[(o, s)][3 * me + q] for o in crossing for q in range(3)], 4)], "qar")
        wait("g", "kar", 16)
        dk = [[match[(s, r)][3 * me + q] for r in range(NR) if r not in group[s]] for q in range(3)]
        send([(ks[0][:], ks[0][:], dk[0], 8)], "kar")
        send([(ks[q][:], ks[q][:], dk[q], 4) for q in (1, 2)], "kar")
        if core == ha:
            for i in range(NP):
                w = T.win[:, PW * i:PW * i + PW]
                wait("g", "b%d" % i, 16)
                send([(w, w, [hb], 16)], "b%d" % i)
    for w in ("P", "V", "S"):
        wait(w, "gs", gm)
    wait("P", "vs", vrep)
    for n, r in enumerate(asked):
        wait("V", "cod%d" % n, 6 * 8)
        c = 16 * n
        G, F, inc, sm = [t[:, c:c + 16] for t in (T.G, T.F, T.inc, T.smap)]
        h2, c1 = T.p1[:, c:c + 16], T.p1[:, 32 + c:48 + c]
        k = did(V.tensor_tensor(h2, T.codes[:, 48 * n:48 * n + 16], T.codes[:, 48 * n + 16:48 * n + 32], A.add), "vs")
        wait("V", "vs", k)
        k = did(V.tensor_tensor(G, h2, T.codes[:, 48 * n + 32:48 * n + 48], A.add), "vs")
        wait("V", "vs", k)
        k = did(V.tensor_scalar(F, G, 0.0, None, A.is_gt), "vs")
        wait("V", "vs", k)
        k = did(V.tensor_tensor_scan(inc, F, zer, 0.0, A.add, A.add), "vs")
        wait("P", "vs", k)
        did(V.tensor_scalar(T.p1[:, 64 + c:80 + c], G, -1.0, None, A.mult), "vs")
        slot = T["r%d" % n][:, 0:16]
        did(PE.matmul(slot, m1[:], F, True, False), "ps")
        p = did(PE.matmul(slot, T.ones[:], inc, False, True), "ps")
        wait("V", "ps", p)
        si = T.si[:, 48 * n:48 * n + 16]
        k1 = did(V.tensor_copy(si, slot), "vs")
        did(V.tensor_scalar(c1, slot, float(CAP * s - ZC), None, A.add), "vs")
        wait("V", "vs", k1)
        did(V.tensor_scalar(T.si[:, 48 * n + 16:48 * n + 32], si, 15, None, A.bitwise_and), "vs")
        k3 = did(V.tensor_scalar(T.si[:, 48 * n + 32:48 * n + 48], si, 4, None, A.arith_shift_right), "vs")
        wait("V", "vs", k3)
        kf = did(V.tensor_copy(T.sf[:, 32 * n:32 * n + 32], T.si[:, 48 * n + 16:48 * n + 48]), "vs")
        km = did(V.tensor_tensor(sm, c1, F, A.mult), "vs")
        wait("V", "vs", kf)
        if r == s:
            wait("Y", "vs", km)
            for h in range(2):
                did(SY.dma_start(T.maps[2 * s + h], T.smap[:, c + 8 * h:c + 8 * h + 8]), "om", 16)
        else:
            wait("g", "vs", km)
            send([(T.smap[:, c + 8 * h:c + 8 * h + 8], T.maps[2 * s + h], [cores[r]], 4) for h in range(2)], "map")
        wait("S", "vs", kf)
        lst = T["r%d" % (2 + n)][0:16, 0:32]
        tv, ts = {}, {}
        for t in range(NT):
            lo, hi = T.sf[:, 32 * n + t:32 * n + t + 1], T.sf[:, 32 * n + 16 + t:32 * n + 17 + t]
            lh = T.lh[:, 256 * n + 16 * t:256 * n + 16 * t + 16]
            rh = T.rh[:, 512 * n + 32 * t:512 * n + 32 * t + 32]
            if t >= NT - SL:
                i = (n * SL + t - NT + SL) * 48
                did(S.activation(T.la2[:, i:i + 16], T.iotap[:, 0:16], AF.Abs, bias=lo, scale=-1.0), "ss")
                a = did(S.activation(T.la2[:, i + 16:i + 48], T.iota32[:], AF.Abs, bias=hi, scale=-1.0), "ss")
                wait("S", "ss", a)
                did(S.activation(lh, T.la2[:, i:i + 16], AF.Relu, bias=1.0, scale=-1.0), "ss")
                ts[t] = did(S.activation(rh, T.la2[:, i + 16:i + 48], AF.Relu, bias=T.G[:, c + t:c + t + 1],
                                         scale=T.p1[:, 64 + c + t:65 + c + t]), "ss")
            else:
                did(V.tensor_scalar(lh, T.iotap[:, 0:16], lo, None, A.is_equal), "vs")
                tv[t] = did(V.tensor_scalar(rh, T.iota32[:], hi, T.G[:, c + t:c + t + 1], A.is_equal, A.mult), "vs")
        for t in range(NT):
            if t in ts:
                wait("P", "ss", ts[t])
            else:
                wait("P", "vs", tv[t])
            p = did(PE.matmul(lst, T.lh[:, 256 * n + 16 * t:256 * n + 16 * t + 16],
                              T.rh[:, 512 * n + 32 * t:512 * n + 32 * t + 32], t == 0, t == NT - 1), "ps")
        wait("V", "ps", p)
        lsb = T.lsb[:, 32 * n:32 * n + 32]
        k = did(V.tensor_copy(lsb, lst), "vs")
        wait("P", "vs", k)
        lst8 = T["r%d" % (4 + n)][:, 0:32]
        p = did(PE.matmul(lst8, T.rep[0:16, :], lsb, True, True), "ps")
        wait("V", "ps", p)
        k = did(V.tensor_scalar(T.off[:, 32 * n:32 * n + 32], lst8, -1.0, None, A.add), "vs")
        for q in ("V", "S"):
            wait(q, "vs", k)
            for i in range(NP):
                wait(q, "%s%d" % ("t" if is_rank else "b", i), 16)
        out = T.ywin if r == s else T.gb
        o = CAP * s if r == s else CAP * n
        kv = did(V.tensor_copy(out[:, o:o + 256], T.win[:, 0:8192].indirect(T.off[:, 32 * n:32 * n + 16])), "vs")
        kc = did(S.activation(out[:, o + 256:o + 512], T.win[:, 0:8192].indirect(T.off[:, 32 * n + 16:32 * n + 32]), AF.Copy), "ss")
        if r != s:
            wait("g", "vs", kv)
            wait("g", "ss", kc)
            send([(T.gb[:, o:o + CAP], T.ywin[:, CAP * s:CAP * s + CAP], [cores[r]], 8)], "dat")
    if not is_rank:
        return
    tot = 8 * (NR - 1)
    wait("Y", "map", tot)
    wait("Y", "om", 32)
    did(SY.dma_start(T.msb[:], T.maps[:]), "ml", 16)
    wait("P", "ml", 16)
    p = did(PE.matmul(T.r6[:, 0:128], T.rep[0:96, :], T.msb[:], True, True), "ps")
    wait("V", "ps", p)
    k = did(V.tensor_scalar(T.yoff[:], T.r6[:, 0:128], float(ZC), None, A.add), "vs")
    for q in ("V", "S"):
        wait(q, "vs", k)
        wait(q, "ss", kc)
        wait(q, "dat", tot)
    for h in range(2):
        a, b = 512 * h, 1024 + 512 * h
        kv = did(V.tensor_copy(T.ysb[:, a:a + 512], T.ywin[:, 0:ZC + 16].indirect(T.yoff[:, 32 * h:32 * h + 32])), "vs")
        kc = did(S.activation(T.ysb[:, b:b + 512], T.ywin[:, 0:ZC + 16].indirect(T.yoff[:, 64 + 32 * h:96 + 32 * h]), AF.Copy), "ss")
        wait("Y", "vs", kv)
        did(SY.dma_start(T.y[:, a:a + 512], T.ysb[:, a:a + 512]), "sy", 16)
        if h == 0:
            wait("Y", "ss", kc)
            did(SY.dma_start(T.y[:, b:b + 512], T.ysb[:, b:b + 512]), "sy", 16)
        else:
            wait("S", "ss", kc)
            did(S.dma_start(T.y[:, b:b + 512], T.ysb[:, b:b + 512]), "sa", 16)


def run_match(g, core, T, topo, role, P, did, wait, send):
    cores, match, gat, jobs, helper, group = P
    s, r, idx = role
    q, h = idx % 3, idx // 3
    n = NK[q]
    nv = n - NS
    V, S, PE, SY = g.vector, g.scalar, g.tensor, g.sync
    ks = [T.ks0, T.ks1, T.ks2][q]
    C_HI, C_LO, C_CODE = 22, 44, 110
    a16, hi16, b1, num, dbl, code, tt = [T.cv[:, 22 * i:22 * i + n] for i in range(7)]
    direct = topo.may_write(cores[r], core)
    wait("S", "qar", 4 // len(parts(ask_direct(topo, cores, match, r, h))) if direct else 4)
    did(S.dma_start(T.Qi[:], T.qh[128 * h:128 * h + 128]), "ql", 16)
    wait("Y", "kar", 4 if q else 8)
    did(SY.dma_start(T.Ki[:, 0:n], ks[:]), "kl", 16)
    did(g.iota(T.pI[:, 0:n], [[0, n]], 0, 1), "gs")
    gi = did(g.iota(tt, [[16, n]], 0, 0, allow_small_or_imprecise_dtypes=True), "gs")
    did(g.iota(T.iota36[:], [[1, 12], [0, 3]], 0, 0, allow_small_or_imprecise_dtypes=True), "gs")
    k = did(V.memset(T.ones[:], 1.0), "vs")
    did(V.memset(T.o256[:], 256.0), "vs")
    kz = did(V.memset(T.zb[:], 0.0), "vs")
    did(V.memset(T.cs[:], 0.0), "vs")
    wait("g", "vs", k)
    gd = did(g.affine_select(T.ident[:], T.ones[:], [[-1, 128]], A.is_equal, 0.0, 0, 1), "gs")
    wait("V", "vs", kz)
    did(V.tensor_copy(T.cls[:], T.zb[:]), "vs")
    wait("V", "gs", gi)
    did(V.tensor_scalar(T.pab[:, 0:n], T.pI[:, 0:n], 7, None, A.bitwise_and), "vs")
    k = did(V.tensor_scalar(T.pab[:, 22:22 + n], T.pI[:, 0:n], 3, None, A.arith_shift_right), "vs")
    wait("V", "vs", k)
    did(V.tensor_copy(T.fab[:, 0:n], T.pab[:, 0:n]), "vs")
    k = did(V.tensor_copy(T.fab[:, 22:22 + n], T.pab[:, 22:22 + n]), "vs")
    wait("V", "vs", k)
    did(V.tensor_scalar(a16, T.fab[:, 0:n], float(16 * n), None, A.mult), "vs")
    k = did(V.tensor_scalar(b1, T.fab[:, 22:22 + n], 1.0, None, A.add), "vs")
    wait("V", "vs", k)
    k = did(V.tensor_tensor(hi16, a16, tt, A.add), "vs")
    wait("V", "vs", k)
    k = did(V.tensor_tensor(num, hi16, b1, A.add), "vs")
    wait("V", "vs", k)
    k = did(V.tensor_scalar(dbl, num, 2.0, -2048.0, A.mult, A.add), "vs")
    wait("V", "vs", k)
    k = did(V.tensor_tensor(code, num, dbl, A.max), "vs")
    wait("V", "vs", k)
    for w in ("V", "S", "P"):
        wait(w, "gs", gd)
    wait("V", "ql", 16)
    did(V.tensor_scalar(T.qq[:, 0:8], T.Qi[:], 255, None, A.bitwise_and), "vs")
    did(V.tensor_scalar(T.qq[:, 8:16], T.Qi[:], 8, 255, A.arith_shift_right, A.bitwise_and), "vs")
    k = did(V.tensor_scalar(T.qq[:, 16:24], T.Qi[:], 16, None, A.arith_shift_right), "vs")
    wait("V", "vs", k)
    k = did(V.tensor_copy(T.qf[:], T.qq[:]), "vs")
    for w in ("V", "S", "P"):
        wait(w, "vs", k)
    vd, sd = {}, {}
    for j in range(NQT):
        vd[j] = did(V.tensor_scalar(T.dl[:, 128 * j:128 * j + 128], T.ident[:], T.qf[:, j:j + 1], None, A.mult), "vs")
        sd[j] = did(S.activation(T.dh[:, 128 * j:128 * j + 128], T.ident[:], AF.Copy, scale=T.qf[:, 8 + j:9 + j]), "ss")
    pb = {}
    for b in range(2):
        bank = T["r%d" % (6 + b)][:]
        wait("P", "vs", vd[4 * b + 3])
        did(PE.matmul(bank, T.ones[:], T.dl[:, 512 * b:512 * b + 512], True, False), "ps")
        wait("P", "ss", sd[4 * b + 3])
        pb[b] = did(PE.matmul(bank, T.o256[:], T.dh[:, 512 * b:512 * b + 512], False, True), "ps")
    wait("V", "kl", 16)
    did(V.tensor_scalar(T.kk[:, 0:n], T.Ki[:, 0:n], 65535, None, A.bitwise_and), "vs")
    k = did(V.tensor_scalar(T.kk[:, 22:22 + n], T.Ki[:, 0:n], 16, None, A.arith_shift_right), "vs")
    wait("V", "vs", k)
    did(V.tensor_copy(T.kf[:, 0:n], T.kk[:, 0:n]), "vs")
    k = did(V.tensor_copy(T.kf[:, 22:22 + n], T.kk[:, 22:22 + n]), "vs")
    wait("V", "vs", k)
    iota12 = T.iota36[:, 0:NC:3]
    cl = {}

    def classes(t):
        hi = T.kf[:, 22 + t:23 + t]
        if t < nv:
            o = NC * t
            cl[t] = did(V.tensor_scalar(T.cls[:, o:o + NC:3], iota12, hi, T.cv[:, C_CODE + t:C_CODE + t + 1], A.is_equal, A.mult), "vs")
        else:
            o = NC * (t - nv)
            did(V.tensor_scalar(T.cs[:, o + 1:o + NC:3], iota12, hi, T.cv[:, C_HI + t:C_HI + t + 1], A.is_equal, A.mult), "vs")
            cl[t] = did(V.tensor_scalar(T.cs[:, o + 2:o + NC:3], iota12, hi, T.cv[:, C_LO + t:C_LO + t + 1], A.is_equal, A.mult), "vs")

    order = list(range(nv))
    for k, at in enumerate((5, 10, 15, nv + 2, nv + 4)):
        order.insert(at, nv + k)
    early, late = order[:9], order[9:]
    for t in early:
        classes(t)
    sc = {}
    for b in range(2):
        bank = T["r%d" % (6 + b)][:]
        wait("V", "ps", pb[b])
        ku = did(V.tensor_copy(T.qu[:, 512 * b:512 * b + 512], bank), "vs")
        wait("S", "vs", ku)
        sc[b] = did(S.activation(T.qs[:, 512 * b:512 * b + 512], bank, AF.Copy), "ss")
    wait("V", "vs", ku)
    wait("S", "ss", sc[1])
    ready = {}
    for t in range(nv):
        ready[t] = ("vs", did(V.tensor_scalar(T.mv[:, 1024 * t:1024 * t + 1024], T.qu[:], T.kf[:, t:t + 1], None, A.is_equal), "vs"))
        for x in late[t:t + 1]:
            classes(x)
    for t in range(nv, n):
        i = 1024 * (t - nv)
        a = did(S.activation(T.ma[:, i:i + 1024], T.qs[:], AF.Abs, bias=T.kf[:, t:t + 1], scale=-1.0), "ss")
        wait("S", "ss", a)
        ready[t] = ("ss", did(S.activation(T.ms[:, i:i + 1024], T.ma[:, i:i + 1024], AF.Relu, bias=1.0, scale=-1.0), "ss"))
    for j in range(NQT):
        km = did(V.tensor_scalar(T.mask[:, NC * j:NC * j + NC], T.iota36[:], T.qf[:, 16 + j:17 + j], None, A.is_equal), "vs")
    for t in order:
        wait("P", ready[t][0], ready[t][1])
        wait("P", "vs", cl[t])
        for j in range(NQT):
            if j >= 6:
                wait("P", "ss", sc[j - 6])
            o = T["r%d" % j][:, 0:NC]
            if t < nv:
                lhs, rhs = T.mv[:, 1024 * t + 128 * j:1024 * t + 128 * j + 128], T.cls[:, NC * t:NC * t + NC]
            else:
                i = t - nv
                lhs, rhs = T.ms[:, 1024 * i + 128 * j:1024 * i + 128 * j + 128], T.cs[:, NC * i:NC * i + NC]
            p = did(PE.matmul(o, lhs, rhs, t == order[0], t == order[-1]), "ps")
    wait("V", "vs", km)
    for j in range(NQT):
        wait("V", "ps", p - NQT + 1 + j)
        k = did(V.tensor_tensor(T.prod[:, j:NQT * NC:NQT], T["r%d" % j][:, 0:NC], T.mask[:, NC * j:NC * j + NC], A.mult), "vs")
    wait("V", "vs", k)
    k = did(V.tensor_tensor(T.p1[:], T.prod[:, 0:144], T.prod[:, 144:288], A.add), "vs")
    wait("V", "vs", k)
    k = did(V.tensor_tensor(T.p2[:], T.p1[:, 0:72], T.p1[:, 72:144], A.add), "vs")
    wait("V", "vs", k)
    k = did(V.tensor_tensor(T.p3[:, 0:24], T.p2[:, 0:24], T.p2[:, 24:48], A.add), "vs")
    wait("V", "vs", k)
    k = did(V.tensor_tensor(T.p3[:, 24:48], T.p3[:, 0:24], T.p2[:, 48:72], A.add), "vs")
    wait("V", "vs", k)
    v, w, f, m, x, y = [T.p3[:, 48 + 8 * i:56 + 8 * i] for i in range(6)]
    num_v = T.p3[:, 24:32]
    did(V.tensor_scalar(w, num_v, 0.5, 1024.0, A.mult, A.add), "vs")
    k = did(V.tensor_tensor(f, T.p3[:, 32:40], T.p3[:, 40:48], A.add), "vs")
    wait("V", "vs", k)
    k = did(V.tensor_tensor(m, num_v, w, A.min), "vs")
    wait("V", "vs", k)
    k = did(V.tensor_tensor(x, m, f, A.add), "vs")
    out = x
    if q:
        wait("V", "vs", k)
        k = did(V.tensor_scalar(v, x, 0.0, float(16 * ST[q]), A.is_gt, A.mult), "vs")
        wait("V", "vs", k)
        k = did(V.tensor_tensor(y, x, v, A.add), "vs")
        out = y
    dst, nth = gat[(s, r)]
    wait("g", "vs", k)
    o = 48 * nth + 16 * q + 8 * h
    send([(out, T.codes[:, o:o + 8], [dst], 8)], "cod%d" % nth)
